import numpy as np
import ml_dtypes


def mxq(x, axis, fmt="e4m3"):
    dtype, down = {"e4m3": (ml_dtypes.float8_e4m3fn, 7), "e5m2": (ml_dtypes.float8_e5m2, 14)}[fmt]
    v = np.moveaxis(np.asarray(x, np.float32).astype(ml_dtypes.bfloat16).astype(np.float64), axis, -1)
    blocks = v.reshape(v.shape[:-1] + (-1, 32))
    amax = np.abs(blocks).max(-1, keepdims=True)
    byte = np.maximum(np.where(amax > 0, np.frexp(amax)[1] - 1 + 127, 0) - down, 1)
    scale = np.exp2(byte - 127.0)
    codes = (blocks / scale).astype(np.float32).astype(dtype).astype(np.float64)
    return np.moveaxis((codes * scale).reshape(v.shape), -1, axis)


WIDE = False


def mx_kscale(k):
    if not WIDE:
        return np.ones(k)
    levels = np.array([10, -10, 5, -5, 0])
    if k % 512:
        return np.exp2(np.random.permutation(np.resize(levels, k // 32))).repeat(32)
    a = np.empty((k // 512, 16))
    for p in range(k // 512):
        a[p, :8] = np.random.permutation(np.resize(levels, 8))
        for g in range(8):
            far = levels[np.abs(levels - a[p, g]) >= 10]
            a[p, g + 8] = far[np.random.randint(len(far))]
    return np.exp2(a.ravel()).repeat(32)


BF16 = ml_dtypes.bfloat16


def bf(x):
    return np.asarray(x, np.float32).astype(BF16)


def f64(x):
    return np.asarray(x).astype(np.float64)


E2M1 = np.array([0.0, 0.5, 1.0, 1.5, 2.0, 3.0, 4.0, 6.0, -0.0, -0.5, -1.0, -1.5, -2.0, -3.0, -4.0, -6.0])


def pack_weight(w, fmt):
    k, n = w.shape
    w = f64(bf(w)).reshape(k // 32, 32, n)
    amax = np.abs(w).max(1)
    if fmt == "e4m3":
        byte = np.frexp(amax)[1] - 1 + 127 - 7
    else:
        mant, ex = np.frexp(amax / 6.0)
        byte = np.where(mant > 0.5, ex, ex - 1) + 127
    byte = np.clip(np.where(amax > 0, byte, 1), 1, 254)
    scaled = (w * np.exp2(127.0 - byte)[:, None, :]).reshape(k, n).astype(np.float32)
    by_word = np.ascontiguousarray(scaled.reshape(k // 512, 128, 4, n).transpose(0, 1, 3, 2))
    if fmt == "e4m3":
        words = by_word.astype(ml_dtypes.float8_e4m3fn).view(np.uint8)
    else:
        c = by_word.astype(ml_dtypes.float4_e2m1fn).view(np.uint8) & 0xF
        words = c[..., 0::2] | (c[..., 1::2] << 4)
    return np.ascontiguousarray(words), np.ascontiguousarray(byte.astype(np.uint8).reshape(k // 512, 16, n))


def unpack_weight(words, scales, fmt):
    g, p, n, _ = words.shape
    if fmt == "e4m3":
        vals = np.ascontiguousarray(words).view(ml_dtypes.float8_e4m3fn).astype(np.float64)
    else:
        nib = np.empty((g, p, n, 4), np.uint8)
        nib[..., 0::2] = words & 0xF
        nib[..., 1::2] = words >> 4
        vals = E2M1[nib]
    vals = vals * np.repeat(np.exp2(scales.astype(np.float64) - 127.0), 8, axis=1)[..., None]
    return vals.transpose(0, 1, 3, 2).reshape(g * 512, n)
def pack4(w):
    words, scales = pack_weight(w, "e2m1")
    return words.reshape(words.shape[0], 128, -1), scales


def unpack4(words, scales):
    return unpack_weight(words.reshape(words.shape[0], 128, -1, 2), scales, "e2m1")


def planes(Y):
    n, m = Y.shape
    b = f64(bf(Y)).reshape(n // 32, 32, m)
    amax = np.abs(b).max(1)
    byte = np.clip(np.where(amax > 0, np.frexp(amax)[1] - 1 + 127 - 7, 1), 1, 254)
    codes = (b * np.exp2(127.0 - byte)[:, None, :]).reshape(n, m).astype(np.float32).astype(ml_dtypes.float8_e4m3fn).view(np.uint8)
    words = codes.reshape(n // 512, 128, 4, m).transpose(0, 1, 3, 2)
    return np.ascontiguousarray(words), np.ascontiguousarray(byte.astype(np.uint8).reshape(n // 512, 16, m))


M, T, A = 1024, 1024, 2048

def setup_inputs():
    s = mx_kscale(T)
    u = mx_kscale(A)
    atoms = np.random.randn(A, T) / np.sqrt(A)
    pinv = np.linalg.pinv(atoms)
    traces = np.random.randn(M, T)
    lam = 0.4 * np.exp(0.2 * np.random.randn(A))
    time_gain = np.exp(0.8 * np.random.randn(T))
    trace_gain = np.exp(0.3 * np.random.randn(M))
    pinv_words, pinv_scales = pack4(pinv / s[:, None] * u[None, :])
    dict_words, dict_scales = pack4(atoms / u[:, None])
    return {
        "traces": bf(traces * s[None, :]),
        "pinv_words": pinv_words,
        "pinv_scales": pinv_scales,
        "lam": bf(lam * u),
        "dict_words": dict_words,
        "dict_scales": dict_scales,
        "time_gain": bf(time_gain),
        "trace_gain": bf(trace_gain),
    }

def reference(traces, pinv_words, pinv_scales, lam, dict_words, dict_scales, time_gain, trace_gain):
    X, L = f64(traces), f64(lam)
    P = unpack4(pinv_words, pinv_scales)
    D = unpack4(dict_words, dict_scales)
    C = mxq(X, 1, "e4m3") @ P
    H = np.sign(C) * np.maximum(np.abs(C) - L[None, :], 0.0)
    R = mxq(H, 1, "e4m3") @ D
    y = R * f64(time_gain)[None, :] * f64(trace_gain)[:, None]
    Y = y.T
    words, scales = planes(Y)
    return y, words, scales

@@ -1,0 +1,628 @@
+from contextlib import ExitStack
+
+import concourse.mybir as mybir
+from concourse.masks import make_identity
+
+F32 = mybir.dt.float32
+BF16 = mybir.dt.bfloat16
+U32 = mybir.dt.uint32
+I32 = mybir.dt.int32
+U8 = mybir.dt.uint8
+FP8X4 = mybir.dt.float8_e4m3fn_x4
+FP4X4 = mybir.dt.float4_e2m1fn_x4
+ALU = mybir.AluOpType
+ACT = mybir.ActivationFunctionType
+
+M, T, A = 1024, 1024, 2048
+P = 128
+FLOPS = 4 * M * T * A
+
+INTER_ON_V = [(0, 3), (0, 2), (1, 3), (1, 2), (2, 3), (3, 3), (3, 2), (3, 1), (4, 3), (5, 3), (5, 2), (6, 3), (7, 0), (7, 1), (7, 2), (7, 3)]
+CAST_ON_V = [(6, 1)]
+ON_G = []
+EMPTY_ON_V = []
+ORDER = [
+    ("neg",),
+    ("turn_x", 0, 0,),
+    ("empty_x", 0, 0,),
+    ("turn_x", 1, 0,),
+    ("empty_x", 1, 0,),
+    ("turn_x", 0, 1,),
+    ("empty_x", 0, 1,),
+    ("turn_x", 1, 1,),
+    ("empty_x", 1, 1,),
+    ("order_p_scales", 0,),
+    ("order_p_scales", 1,),
+    ("order_p_words", 0, 0,),
+    ("order_p_scales", 2,),
+    ("quant_x", 0, 0,),
+    ("order_p_words", 0, 1,),
+    ("order_p_scales", 3,),
+    ("quant_x", 0, 1,),
+    ("order_p_words", 1, 0,),
+    ("order_p_words", 1, 1,),
+    ("codes_pass", 0, 0,),
+    ("codes_pass", 1, 0,),
+    ("codes_pass", 2, 0,),
+    ("codes_pass", 3, 0,),
+    ("codes_pass", 0, 1,),
+    ("relu", 0,),
+    ("codes_pass", 1, 1,),
+    ("relu", 1,),
+    ("codes_pass", 2, 1,),
+    ("relu", 2,),
+    ("codes_pass", 3, 1,),
+    ("shrink", 0,),
+    ("relu", 3,),
+    ("codes_pass", 4, 0,),
+    ("codes_pass", 4, 1,),
+    ("order_p_words", 2, 1,),
+    ("shrink", 1,),
+    ("order_p_words", 2, 0,),
+    ("relu", 4,),
+    ("codes_pass", 5, 0,),
+    ("codes_pass", 5, 1,),
+    ("shrink", 2,),
+    ("relu", 5,),
+    ("codes_pass", 6, 0,),
+    ("codes_pass", 6, 1,),
+    ("turn_x", 2, 1,),
+    ("turn_x", 3, 1,),
+    ("empty_x", 2, 1,),
+    ("shrink", 3,),
+    ("relu", 6,),
+    ("codes_pass", 7, 0,),
+    ("codes_pass", 7, 1,),
+    ("order_p_words", 3, 1,),
+    ("shrink", 4,),
+    ("empty_x", 3, 1,),
+    ("order_p_words", 3, 0,),
+    ("relu", 7,),
+    ("codes_pass", 8, 0,),
+    ("codes_pass", 8, 1,),
+    ("shrink", 5,),
+    ("interleave", 0, 1,),
+    ("interleave", 0, 0,),
+    ("relu", 8,),
+    ("codes_pass", 9, 0,),
+    ("codes_pass", 9, 1,),
+    ("shrink", 6,),
+    ("relu", 9,),
+    ("codes_pass", 10, 0,),
+    ("codes_pass", 10, 1,),
+    ("interleave", 0, 3,),
+    ("interleave", 0, 2,),
+    ("shrink", 7,),
+    ("turn_x", 2, 0,),
+    ("turn_x", 3, 0,),
+    ("empty_x", 2, 0,),
+    ("quant_h", 0,),
+    ("quant_x", 1, 1,),
+    ("relu", 10,),
+    ("codes_pass", 11, 0,),
+    ("codes_pass", 11, 1,),
+    ("shrink", 8,),
+    ("empty_x", 3, 0,),
+    ("quant_x", 1, 0,),
+    ("relu", 11,),
+    ("codes_pass", 12, 0,),
+    ("codes_pass", 12, 1,),
+    ("shrink", 9,),
+    ("interleave", 1, 1,),
+    ("interleave", 1, 0,),
+    ("relu", 12,),
+    ("codes_pass", 13, 0,),
+    ("codes_pass", 13, 1,),
+    ("shrink", 10,),
+    ("relu", 13,),
+    ("codes_pass", 14, 0,),
+    ("codes_pass", 14, 1,),
+    ("interleave", 1, 3,),
+    ("interleave", 1, 2,),
+    ("shrink", 11,),
+    ("quant_h", 1,),
+    ("relu", 14,),
+    ("codes_pass", 15, 0,),
+    ("codes_pass", 15, 1,),
+    ("shrink", 12,),
+    ("relu", 15,),
+    ("codes_pass", 16, 0,),
+    ("codes_pass", 16, 1,),
+    ("shrink", 13,),
+    ("interleave", 2, 2,),
+    ("interleave", 2, 1,),
+    ("interleave", 2, 0,),
+    ("relu", 16,),
+    ("codes_pass", 17, 0,),
+    ("codes_pass", 17, 1,),
+    ("shrink", 14,),
+    ("relu", 17,),
+    ("codes_pass", 18, 0,),
+    ("codes_pass", 18, 1,),
+    ("interleave", 2, 3,),
+    ("shrink", 15,),
+    ("quant_h", 2,),
+    ("relu", 18,),
+    ("codes_pass", 19, 0,),
+    ("codes_pass", 19, 1,),
+    ("shrink", 16,),
+    ("relu", 19,),
+    ("codes_pass", 20, 0,),
+    ("codes_pass", 20, 1,),
+    ("shrink", 17,),
+    ("interleave", 3, 0,),
+    ("relu", 20,),
+    ("codes_pass", 21, 0,),
+    ("codes_pass", 21, 1,),
+    ("shrink", 18,),
+    ("relu", 21,),
+    ("interleave", 3, 3,),
+    ("codes_pass", 22, 0,),
+    ("codes_pass", 22, 1,),
+    ("interleave", 3, 2,),
+    ("interleave", 3, 1,),
+    ("rebuild_pass", 0, 0, 0,),
+    ("rebuild_pass", 0, 0, 1,),
+    ("rebuild_pass", 0, 0, 2,),
+    ("rebuild_pass", 1, 0, 0,),
+    ("rebuild_pass", 1, 0, 1,),
+    ("rebuild_pass", 1, 0, 2,),
+    ("shrink", 19,),
+    ("quant_h", 3,),
+    ("relu", 22,),
+    ("codes_pass", 23, 0,),
+    ("codes_pass", 23, 1,),
+    ("shrink", 20,),
+    ("interleave", 4, 2,),
+    ("interleave", 4, 1,),
+    ("interleave", 4, 0,),
+    ("relu", 23,),
+    ("codes_pass", 24, 0,),
+    ("codes_pass", 24, 1,),
+    ("shrink", 21,),
+    ("relu", 24,),
+    ("codes_pass", 25, 0,),
+    ("codes_pass", 25, 1,),
+    ("rebuild_pass", 1, 0, 3,),
+    ("interleave", 4, 3,),
+    ("shrink", 22,),
+    ("rebuild_pass", 0, 0, 3,),
+    ("quant_h", 4,),
+    ("relu", 25,),
+    ("codes_pass", 26, 0,),
+    ("codes_pass", 26, 1,),
+    ("shrink", 23,),
+    ("relu", 26,),
+    ("codes_pass", 27, 0,),
+    ("codes_pass", 27, 1,),
+    ("shrink", 24,),
+    ("interleave", 5, 1,),
+    ("interleave", 5, 0,),
+    ("rebuild_pass", 0, 1, 0,),
+    ("rebuild_pass", 0, 1, 1,),
+    ("rebuild_pass", 0, 1, 2,),
+    ("rebuild_pass", 0, 1, 3,),
+    ("relu", 27,),
+    ("codes_pass", 28, 0,),
+    ("codes_pass", 28, 1,),
+    ("shrink", 25,),
+    ("relu", 28,),
+    ("rebuild_pass", 1, 1, 0,),
+    ("rebuild_pass", 1, 1, 1,),
+    ("rebuild_pass", 1, 1, 2,),
+    ("rebuild_pass", 1, 1, 3,),
+    ("gain", 1, 0,),
+    ("codes_pass", 29, 0,),
+    ("codes_pass", 29, 1,),
+    ("interleave", 5, 3,),
+    ("interleave", 5, 2,),
+    ("shrink", 26,),
+    ("gain", 0, 0,),
+    ("cast_y", 1, 0,),
+    ("quant_h", 5,),
+    ("relu", 29,),
+    ("cast_y", 0, 0,),
+    ("rebuild_pass", 2, 0, 0,),
+    ("rebuild_pass", 2, 0, 1,),
+    ("rebuild_pass", 2, 0, 2,),
+    ("rebuild_pass", 2, 0, 3,),
+    ("codes_pass", 30, 0,),
+    ("codes_pass", 30, 1,),
+    ("shrink", 27,),
+    ("relu", 30,),
+    ("rebuild_pass", 3, 0, 0,),
+    ("rebuild_pass", 3, 0, 1,),
+    ("rebuild_pass", 3, 0, 2,),
+    ("rebuild_pass", 3, 0, 3,),
+    ("codes_pass", 31, 0,),
+    ("codes_pass", 31, 1,),
+    ("shrink", 28,),
+    ("gain", 0, 1,),
+    ("interleave", 6, 2,),
+    ("interleave", 6, 1,),
+    ("interleave", 6, 0,),
+    ("relu", 31,),
+    ("cast_y", 0, 1,),
+    ("rebuild_pass", 2, 1, 0,),
+    ("rebuild_pass", 2, 1, 1,),
+    ("rebuild_pass", 2, 1, 2,),
+    ("rebuild_pass", 2, 1, 3,),
+    ("shrink", 29,),
+    ("gain", 1, 1,),
+    ("cast_y", 1, 1,),
+    ("interleave", 6, 3,),
+    ("rebuild_pass", 3, 1, 0,),
+    ("rebuild_pass", 3, 1, 1,),
+    ("rebuild_pass", 3, 1, 2,),
+    ("rebuild_pass", 3, 1, 3,),
+    ("shrink", 30,),
+    ("quant_h", 6,),
+    ("gain", 2, 0,),
+    ("cast_y", 2, 0,),
+    ("shrink", 31,),
+    ("gain", 3, 0,),
+    ("cast_y", 3, 0,),
+    ("gain", 2, 1,),
+    ("cast_y", 2, 1,),
+    ("gain", 3, 1,),
+    ("interleave", 7, 0,),
+    ("rebuild_pass", 4, 0, 0,),
+    ("rebuild_pass", 4, 0, 1,),
+    ("rebuild_pass", 4, 0, 2,),
+    ("rebuild_pass", 5, 0, 0,),
+    ("rebuild_pass", 5, 0, 1,),
+    ("rebuild_pass", 5, 0, 2,),
+    ("rebuild_pass", 4, 1, 0,),
+    ("rebuild_pass", 4, 1, 1,),
+    ("rebuild_pass", 4, 1, 2,),
+    ("rebuild_pass", 5, 1, 0,),
+    ("rebuild_pass", 5, 1, 1,),
+    ("rebuild_pass", 5, 1, 2,),
+    ("cast_y", 3, 1,),
+    ("interleave", 7, 1,),
+    ("turn_y", 0, 2, 0,),
+    ("turn_y", 0, 2, 1,),
+    ("interleave", 7, 2,),
+    ("interleave", 7, 3,),
+    ("turn_y", 2, 2, 0,),
+    ("turn_y", 2, 2, 1,),
+    ("quant_h", 7,),
+    ("empty_y", 0, 2, 0,),
+    ("empty_y", 0, 2, 1,),
+    ("empty_y", 2, 2, 0,),
+    ("empty_y", 2, 2, 1,),
+    ("rebuild_pass", 6, 0, 0,),
+    ("rebuild_pass", 6, 0, 1,),
+    ("rebuild_pass", 6, 0, 2,),
+    ("rebuild_pass", 6, 0, 3,),
+    ("rebuild_pass", 5, 1, 3,),
+    ("rebuild_pass", 4, 1, 3,),
+    ("quant_y", 0, 2, 0,),
+    ("quant_y", 0, 2, 1,),
+    ("rebuild_pass", 5, 0, 3,),
+    ("rebuild_pass", 4, 0, 3,),
+    ("rebuild_pass", 7, 0, 0,),
+    ("rebuild_pass", 7, 0, 1,),
+    ("rebuild_pass", 7, 0, 2,),
+    ("rebuild_pass", 7, 0, 3,),
+    ("quant_y", 2, 2, 0,),
+    ("quant_y", 2, 2, 1,),
+    ("rebuild_pass", 6, 1, 0,),
+    ("rebuild_pass", 6, 1, 1,),
+    ("rebuild_pass", 6, 1, 2,),
+    ("rebuild_pass", 6, 1, 3,),
+    ("rebuild_pass", 7, 1, 0,),
+    ("rebuild_pass", 7, 1, 1,),
+    ("rebuild_pass", 7, 1, 2,),
+    ("rebuild_pass", 7, 1, 3,),
+    ("gain", 6, 0,),
+    ("gain", 5, 1,),
+    ("gain", 4, 1,),
+    ("gain", 5, 0,),
+    ("cast_y", 6, 0,),
+    ("gain", 4, 0,),
+    ("gain", 7, 0,),
+    ("cast_y", 5, 1,),
+    ("cast_y", 4, 1,),
+    ("turn_y", 4, 2, 1,),
+    ("cast_y", 5, 0,),
+    ("cast_y", 4, 0,),
+    ("turn_y", 4, 2, 0,),
+    ("cast_y", 7, 0,),
+    ("turn_y", 6, 2, 0,),
+    ("gain", 6, 1,),
+    ("cast_y", 6, 1,),
+    ("turn_y", 6, 1, 1,),
+    ("gain_bf", 7, 1,),
+    ("gain", 7, 1,),
+    ("turn_y", 7, 1, 1,),
+    ("empty_y", 4, 2, 1,),
+    ("empty_y", 4, 2, 0,),
+    ("empty_y", 6, 2, 0,),
+    ("empty_y", 6, 1, 1,),
+    ("empty_y", 7, 1, 1,),
+    ("quant_y", 4, 2, 1,),
+    ("quant_y", 4, 2, 0,),
+    ("quant_y", 6, 2, 0,),
+    ("store_scales", 0,),
+    ("quant_y", 6, 1, 1,),
+    ("quant_y", 7, 1, 1,),
+]
+
+
+def tile_pinv_shrink_seismic_traces_h1_kernel(
+    tc, traces, pinv_words, pinv_scales, lam, dict_words, dict_scales, time_gain, trace_gain, out_0, out_1, out_2
+):
+    nc = tc.nc
+    with ExitStack() as ctx:
+        sb = ctx.enter_context(tc.tile_pool(name="sb", bufs=1))
+        pp = ctx.enter_context(tc.psum_pool(name="pp", bufs=1))
+        ctx.enter_context(tc.manual_schedule())
+
+        def tiles(name, count, shape, dtype):
+            return [sb.tile(shape, dtype, name="%s%d" % (name, k), align_bytes=64) for k in range(count)]
+
+        banks = [pp.tile([P, 512], F32, name="bank%d" % k) for k in range(8)]
+        free_banks = list(range(8))
+
+        ident = sb.tile([P, P], F32, name="ident", align_bytes=64)
+        x_raw = tiles("x_raw", 8, [P, 2, 512], BF16)
+        x_grp = tiles("x_grp", 4, [P, 2048], BF16)
+        x_codes = tiles("x_codes", 4, [P, 512], U32)
+        x_scales = tiles("x_scales", 4, [P, 512], U8)
+        p_raw = tiles("p_raw", 4, [P, 2, 1024], U8)
+        p_words = tiles("p_words", 4, [P, 2, 1024], U8)
+        ps_raw = sb.tile([P, 2, A], U8, name="ps_raw", align_bytes=64)
+        p_scales = tiles("p_scales", 4, [P, 2, 512], U8)
+        d_words = tiles("d_words", 4, [P, 2048], U8)
+        d_scales = sb.tile([P, 4, T], U8, name="d_scales", align_bytes=64)
+        lam_sb = sb.tile([P, 16], BF16, name="lam_sb", align_bytes=64)
+        neg_lam = sb.tile([P, 16], F32, name="neg_lam", align_bytes=64)
+        tg = sb.tile([P, T], BF16, name="tg", align_bytes=64)
+        trg = sb.tile([P, 8, 2], BF16, name="trg", align_bytes=64)
+        upper = tiles("upper", 4, [P, 512], BF16)
+        h_rows = tiles("h_rows", 3, [P, 4, 512], BF16)
+        h_grp = tiles("h_grp", 3, [P, 2048], BF16)
+        h_codes = tiles("h_codes", 8, [P, 512], U32)
+        h_scales = tiles("h_scales", 8, [P, 512], U8)
+        y = tiles("y", 16, [P, 512], F32)
+        y_bf = tiles("y_bf", 16, [P, 512], BF16)
+        y_grp = tiles("y_grp", 4, [P, 1024], BF16)
+        y_codes = sb.tile([P, 2, M], U32, name="y_codes", align_bytes=64)
+        y_scales = sb.tile([P, 2, M], U8, name="y_scales", align_bytes=64)
+
+        held = {}
+
+        def take(key):
+            held[key] = free_banks[0]
+            free_banks.remove(held[key])
+            return banks[held[key]]
+
+        def give(key):
+            free_banks.append(held[key])
+            return banks[held[key]]
+
+        def load_x(b, g):
+            src = traces[256 * b : 256 * (b + 1), 512 * g : 512 * (g + 1)]
+            nc.sync.dma_start(out=x_raw[2 * b + g][:], in_=src.rearrange("(e p) c -> p e c", p=P))
+
+        def load_p(a):
+            src = pinv_words[:, :, 1024 * a : 1024 * (a + 1)].rearrange("g p c -> p g c")
+            nc.sync.dma_start(out=p_raw[a][:].bitcast(I32), in_=src.bitcast(I32))
+
+        def load_scales(plane, scales):
+            for q in range(4):
+                src = scales[:, 4 * q : 4 * q + 4, :].rearrange("g r c -> r g c")
+                nc.sync.dma_start(out=plane[32 * q : 32 * q + 4, :, :].bitcast(I32), in_=src.bitcast(I32))
+
+        def load_d(a):
+            nc.sync.dma_start(out=d_words[a][:].bitcast(I32), in_=dict_words[a].bitcast(I32))
+
+        def turn_x(b, g):
+            bank = take(("x", b, g))
+            words = x_raw[2 * b + g][:].rearrange("p e c -> p (e c)").bitcast(F32)
+            for e in range(2):
+                for u in range(2):
+                    k = 2 * e + u
+                    nc.tensor.transpose(bank[:, P * k : P * (k + 1)], words[:, 256 * e + u : 256 * (e + 1) : 2], ident[:])
+
+        def empty_x(b, g):
+            bank = give(("x", b, g))
+            dst = x_grp[2 * (b // 2) + g][:].bitcast(F32)[:, 512 * (b % 2) : 512 * (b % 2 + 1)]
+            copy = nc.vector.tensor_copy if ("x", b, g) in EMPTY_ON_V else nc.scalar.copy
+            copy(
+                out=dst.rearrange("p (e m u) -> p e m u", e=2, u=2),
+                in_=bank[:].rearrange("p (e u m) -> p e m u", e=2, u=2),
+            )
+
+        def quant_x(h, g):
+            k = 2 * h + g
+            nc.vector.quantize_mx(out=x_codes[k][:].bitcast(FP8X4), scales=x_scales[k][:], in_=x_grp[k][:])
+
+        def order_p_words(a, g):
+            nc.vector.tensor_copy(
+                out=p_words[a][:, g, :].rearrange("p (j m e) -> p j m e", j=4, e=2),
+                in_=p_raw[a][:, g, :].rearrange("p (m j e) -> p j m e", j=4, e=2),
+            )
+
+        def order_p_scales(a):
+            nc.vector.tensor_copy(
+                out=p_scales[a][:].rearrange("p g (j m) -> p g j m", j=4),
+                in_=ps_raw[:, :, 512 * a : 512 * (a + 1)].rearrange("p g (m j) -> p g j m", j=4),
+            )
+
+        def codes_pass(s, g):
+            h, a, j = s // 16, (s // 4) % 4, s % 4
+            bank = take(("c", s)) if g == 0 else banks[held[("c", s)]]
+            nc.tensor.matmul_mx(
+                out=bank[:],
+                lhsT=p_words[a][:, g, 256 * j : 256 * (j + 1)].bitcast(FP4X4),
+                lhsT_scale=p_scales[a][:, g, P * j : P * (j + 1)],
+                rhs=x_codes[2 * h + g][:].bitcast(FP8X4),
+                rhs_scale=x_scales[2 * h + g][:],
+                start=(g == 0),
+                stop=(g == 1),
+            )
+
+        def neg():
+            nc.scalar.activation(out=neg_lam[:], in_=lam_sb[:], func=ACT.Copy, scale=-1.0)
+
+        def relu(s):
+            col = s % 16
+            bank = banks[held[("c", s)]]
+            nc.scalar.activation(
+                out=upper[s % 4][:], in_=bank[:], func=ACT.Relu, bias=neg_lam[:, col : col + 1], scale=1.0
+            )
+
+        def shrink(s):
+            n, j = s // 4, s % 4
+            col = s % 16
+            bank = give(("c", s))
+            nc.vector.scalar_tensor_tensor(
+                out=h_rows[n % 3][:, j, :],
+                in0=bank[:],
+                scalar=lam_sb[:, col : col + 1],
+                in1=upper[s % 4][:],
+                op0=ALU.add,
+                op1=ALU.min,
+            )
+
+        def interleave(n, q):
+            dst = h_grp[n % 3][:, 512 * q : 512 * (q + 1)].rearrange("p (c i t) -> p c t i", i=4, t=4)
+            src = h_rows[n % 3][:, :, P * q : P * (q + 1)].rearrange("p t (c i) -> p c t i", i=4)
+            if ("i", n, q) in ON_G:
+                src = h_rows[n % 3][:, :, P * q : P * (q + 1)].rearrange("p t c -> p c t")
+                dst = h_grp[n % 3][:, 512 * q : 512 * (q + 1)].rearrange("p (c t) -> p c t", t=4)
+                nc.gpsimd.tensor_scalar(out=dst, in0=src, scalar1=1.0, scalar2=0.0, op0=ALU.mult, op1=ALU.add)
+            elif (n, q) in INTER_ON_V:
+                nc.vector.tensor_copy(out=dst, in_=src)
+            else:
+                nc.scalar.copy(out=dst, in_=src)
+
+        def quant_h(n):
+            nc.vector.quantize_mx(out=h_codes[n][:].bitcast(FP8X4), scales=h_scales[n][:], in_=h_grp[n % 3][:])
+
+        def rebuild_pass(i, g, a):
+            bank = take(("r", i, g)) if a == 0 else banks[held[("r", i, g)]]
+            n = 4 * (i // 4) + a
+            cols = slice(P * (i % 4), P * (i % 4 + 1))
+            nc.tensor.matmul_mx(
+                out=bank[:],
+                lhsT=h_codes[n][:, cols].bitcast(FP8X4),
+                lhsT_scale=h_scales[n][:, cols],
+                rhs=d_words[a][:, 1024 * g : 1024 * (g + 1)].bitcast(FP4X4),
+                rhs_scale=d_scales[:, a, 512 * g : 512 * (g + 1)],
+                start=(a == 0),
+                stop=(a == 3),
+            )
+
+        def apply_gains(i, g, dst):
+            nc.vector.scalar_tensor_tensor(
+                out=dst,
+                in0=banks[held[("r", i, g)]][:],
+                scalar=trg[:, i, 0:1],
+                in1=tg[:, 512 * g : 512 * (g + 1)],
+                op0=ALU.mult,
+                op1=ALU.mult,
+            )
+
+        def gain(i, g):
+            apply_gains(i, g, y[2 * i + g][:])
+            give(("r", i, g))
+            nc.sync.dma_start(out=out_0[P * i : P * (i + 1), 512 * g : 512 * (g + 1)], in_=y[2 * i + g][:])
+
+        def gain_bf(i, g):
+            apply_gains(i, g, y_bf[2 * i + g][:])
+
+        def cast_y(i, g):
+            dst = y_bf[2 * i + g][:].rearrange("p (u w e) -> p u w e", u=2, e=2)
+            src = y[2 * i + g][:].rearrange("p (w u e) -> p u w e", u=2, e=2)
+            if ("c", i, g) in ON_G:
+                nc.gpsimd.tensor_scalar(out=dst, in0=src, scalar1=1.0, scalar2=0.0, op0=ALU.mult, op1=ALU.add)
+            elif (i, g) in CAST_ON_V:
+                nc.vector.tensor_copy(out=dst, in_=src)
+            else:
+                nc.scalar.copy(out=dst, in_=src)
+
+        def turn_y(i, count, g):
+            bank = take(("y", i, g))
+            for e in range(count):
+                words = y_bf[2 * (i + e) + g][:].bitcast(F32)
+                for u in range(2):
+                    k = 2 * e + u
+                    src = words[:, u:256:2] if (i + e, g) == (7, 1) else words[:, P * u : P * (u + 1)]
+                    nc.tensor.transpose(bank[:, P * k : P * (k + 1)], src, ident[:])
+
+        def y_stage(i, count, g):
+            return y_grp[(2 * (i // 2) + g) % 4][:, 512 * (i % 2) : 512 * (i % 2 + count)]
+
+        def empty_y(i, count, g):
+            bank = give(("y", i, g))
+            copy = nc.vector.tensor_copy if ("y", i, g) in EMPTY_ON_V else nc.scalar.copy
+            copy(
+                out=y_stage(i, count, g).bitcast(F32).rearrange("p (e m u) -> p e m u", e=count, u=2),
+                in_=bank[:, 0 : 256 * count].rearrange("p (e u m) -> p e m u", e=count, u=2),
+            )
+
+        def quant_y(i, count, g):
+            cols = slice(P * i, P * (i + count))
+            nc.vector.quantize_mx(
+                out=y_codes[:, g, cols].bitcast(FP8X4), scales=y_scales[:, g, cols], in_=y_stage(i, count, g)
+            )
+            dst = out_1[g, :, cols, :].rearrange("p m t -> p (m t)")
+            nc.sync.dma_start(out=dst.bitcast(I32), in_=y_codes[:, g, cols].bitcast(I32))
+
+        def store_scales(g):
+            for q in range(4):
+                queue = nc.sync if (g == 0 or q < 2) else nc.scalar
+                dst = out_2[g, 4 * q : 4 * q + 4, :]
+                queue.dma_start(out=dst.bitcast(I32), in_=y_scales[32 * q : 32 * q + 4, g, :].bitcast(I32))
+
+        nc.vector.memset(ps_raw[:].rearrange("p g c -> p (g c)").bitcast(I32), 0)
+        make_identity(nc, ident[:])
+        nc.gpsimd.memset(d_scales[:].rearrange("p g c -> p (g c)").bitcast(I32), 0)
+        load_x(0, 0)
+        nc.sync.dma_start(
+            out=lam_sb[:].rearrange("p (a j) -> p a j", j=4), in_=lam.rearrange("(a p j) -> p a j", p=P, j=4)
+        )
+        load_scales(ps_raw, pinv_scales)
+        load_x(1, 0)
+        load_p(0)
+        load_x(0, 1)
+        load_x(1, 1)
+        load_p(1)
+        for g in (1, 0):
+            for b in range(2, 4):
+                load_x(b, g)
+            load_p(3 - g)
+        load_scales(d_scales, dict_scales)
+        for a in range(4):
+            load_d(a)
+        nc.sync.dma_start(out=tg[:], in_=time_gain.partition_broadcast(P))
+        with nc.allow_non_contiguous_dma(reason="one gain for each partition"):
+            nc.sync.dma_start(out=trg[:, :, 0:1], in_=trace_gain.rearrange("(i p o) -> p i o", p=P, o=1))
+
+        table = {
+            "turn_x": turn_x,
+            "empty_x": empty_x,
+            "quant_x": quant_x,
+            "order_p_words": order_p_words,
+            "order_p_scales": order_p_scales,
+            "neg": neg,
+            "codes_pass": codes_pass,
+            "relu": relu,
+            "shrink": shrink,
+            "interleave": interleave,
+            "quant_h": quant_h,
+            "rebuild_pass": rebuild_pass,
+            "gain": gain,
+            "gain_bf": gain_bf,
+            "cast_y": cast_y,
+            "turn_y": turn_y,
+            "empty_y": empty_y,
+            "quant_y": quant_y,
+            "store_scales": store_scales,
+        }
+        for step in ORDER:
+            table[step[0]](*step[1:])
+        store_scales(1)

@@ -17,336 +17,319 @@ M, T, A = 1024, 1024, 2048
 P = 128
 FLOPS = 4 * M * T * A
 
-INTER_ON_V = [(0, 3), (0, 2), (1, 3), (1, 2), (2, 3), (3, 3), (3, 2), (3, 1), (4, 3), (5, 3), (5, 2), (6, 3), (7, 0), (7, 1), (7, 2), (7, 3)]
-CAST_ON_V = [(6, 1)]
-ON_G = []
-EMPTY_ON_V = []
 ORDER = [
-    ("neg",),
-    ("turn_x", 0, 0,),
-    ("empty_x", 0, 0,),
-    ("turn_x", 1, 0,),
-    ("empty_x", 1, 0,),
-    ("turn_x", 0, 1,),
-    ("empty_x", 0, 1,),
-    ("turn_x", 1, 1,),
-    ("empty_x", 1, 1,),
-    ("order_p_scales", 0,),
-    ("order_p_scales", 1,),
-    ("order_p_words", 0, 0,),
-    ("order_p_scales", 2,),
-    ("quant_x", 0, 0,),
-    ("order_p_words", 0, 1,),
-    ("order_p_scales", 3,),
-    ("quant_x", 0, 1,),
-    ("order_p_words", 1, 0,),
-    ("order_p_words", 1, 1,),
-    ("codes_pass", 0, 0,),
-    ("codes_pass", 1, 0,),
-    ("codes_pass", 2, 0,),
-    ("codes_pass", 3, 0,),
-    ("codes_pass", 0, 1,),
-    ("relu", 0,),
-    ("codes_pass", 1, 1,),
-    ("relu", 1,),
-    ("codes_pass", 2, 1,),
-    ("relu", 2,),
-    ("codes_pass", 3, 1,),
-    ("shrink", 0,),
-    ("relu", 3,),
-    ("codes_pass", 4, 0,),
-    ("codes_pass", 4, 1,),
-    ("order_p_words", 2, 1,),
-    ("shrink", 1,),
-    ("order_p_words", 2, 0,),
-    ("relu", 4,),
-    ("codes_pass", 5, 0,),
-    ("codes_pass", 5, 1,),
-    ("shrink", 2,),
-    ("relu", 5,),
-    ("codes_pass", 6, 0,),
-    ("codes_pass", 6, 1,),
-    ("turn_x", 2, 1,),
-    ("turn_x", 3, 1,),
-    ("empty_x", 2, 1,),
-    ("shrink", 3,),
-    ("relu", 6,),
-    ("codes_pass", 7, 0,),
-    ("codes_pass", 7, 1,),
-    ("order_p_words", 3, 1,),
-    ("shrink", 4,),
-    ("empty_x", 3, 1,),
-    ("order_p_words", 3, 0,),
-    ("relu", 7,),
-    ("codes_pass", 8, 0,),
-    ("codes_pass", 8, 1,),
-    ("shrink", 5,),
-    ("interleave", 0, 1,),
-    ("interleave", 0, 0,),
-    ("relu", 8,),
-    ("codes_pass", 9, 0,),
-    ("codes_pass", 9, 1,),
-    ("shrink", 6,),
-    ("relu", 9,),
-    ("codes_pass", 10, 0,),
-    ("codes_pass", 10, 1,),
-    ("interleave", 0, 3,),
-    ("interleave", 0, 2,),
-    ("shrink", 7,),
-    ("turn_x", 2, 0,),
-    ("turn_x", 3, 0,),
-    ("empty_x", 2, 0,),
-    ("quant_h", 0,),
-    ("quant_x", 1, 1,),
-    ("relu", 10,),
-    ("codes_pass", 11, 0,),
-    ("codes_pass", 11, 1,),
-    ("shrink", 8,),
-    ("empty_x", 3, 0,),
-    ("quant_x", 1, 0,),
-    ("relu", 11,),
-    ("codes_pass", 12, 0,),
-    ("codes_pass", 12, 1,),
-    ("shrink", 9,),
-    ("interleave", 1, 1,),
-    ("interleave", 1, 0,),
-    ("relu", 12,),
-    ("codes_pass", 13, 0,),
-    ("codes_pass", 13, 1,),
-    ("shrink", 10,),
-    ("relu", 13,),
-    ("codes_pass", 14, 0,),
-    ("codes_pass", 14, 1,),
-    ("interleave", 1, 3,),
-    ("interleave", 1, 2,),
-    ("shrink", 11,),
-    ("quant_h", 1,),
-    ("relu", 14,),
-    ("codes_pass", 15, 0,),
-    ("codes_pass", 15, 1,),
-    ("shrink", 12,),
-    ("relu", 15,),
-    ("codes_pass", 16, 0,),
-    ("codes_pass", 16, 1,),
-    ("shrink", 13,),
-    ("interleave", 2, 2,),
-    ("interleave", 2, 1,),
-    ("interleave", 2, 0,),
-    ("relu", 16,),
-    ("codes_pass", 17, 0,),
-    ("codes_pass", 17, 1,),
-    ("shrink", 14,),
-    ("relu", 17,),
-    ("codes_pass", 18, 0,),
-    ("codes_pass", 18, 1,),
-    ("interleave", 2, 3,),
-    ("shrink", 15,),
-    ("quant_h", 2,),
-    ("relu", 18,),
-    ("codes_pass", 19, 0,),
-    ("codes_pass", 19, 1,),
-    ("shrink", 16,),
-    ("relu", 19,),
-    ("codes_pass", 20, 0,),
-    ("codes_pass", 20, 1,),
-    ("shrink", 17,),
-    ("interleave", 3, 0,),
-    ("relu", 20,),
-    ("codes_pass", 21, 0,),
-    ("codes_pass", 21, 1,),
-    ("shrink", 18,),
-    ("relu", 21,),
-    ("interleave", 3, 3,),
-    ("codes_pass", 22, 0,),
-    ("codes_pass", 22, 1,),
-    ("interleave", 3, 2,),
-    ("interleave", 3, 1,),
-    ("rebuild_pass", 0, 0, 0,),
-    ("rebuild_pass", 0, 0, 1,),
-    ("rebuild_pass", 0, 0, 2,),
-    ("rebuild_pass", 1, 0, 0,),
-    ("rebuild_pass", 1, 0, 1,),
-    ("rebuild_pass", 1, 0, 2,),
-    ("shrink", 19,),
-    ("quant_h", 3,),
-    ("relu", 22,),
-    ("codes_pass", 23, 0,),
-    ("codes_pass", 23, 1,),
-    ("shrink", 20,),
-    ("interleave", 4, 2,),
-    ("interleave", 4, 1,),
-    ("interleave", 4, 0,),
-    ("relu", 23,),
-    ("codes_pass", 24, 0,),
-    ("codes_pass", 24, 1,),
-    ("shrink", 21,),
-    ("relu", 24,),
-    ("codes_pass", 25, 0,),
-    ("codes_pass", 25, 1,),
-    ("rebuild_pass", 1, 0, 3,),
-    ("interleave", 4, 3,),
-    ("shrink", 22,),
-    ("rebuild_pass", 0, 0, 3,),
-    ("quant_h", 4,),
-    ("relu", 25,),
-    ("codes_pass", 26, 0,),
-    ("codes_pass", 26, 1,),
-    ("shrink", 23,),
-    ("relu", 26,),
-    ("codes_pass", 27, 0,),
-    ("codes_pass", 27, 1,),
-    ("shrink", 24,),
-    ("interleave", 5, 1,),
-    ("interleave", 5, 0,),
-    ("rebuild_pass", 0, 1, 0,),
-    ("rebuild_pass", 0, 1, 1,),
-    ("rebuild_pass", 0, 1, 2,),
-    ("rebuild_pass", 0, 1, 3,),
-    ("relu", 27,),
-    ("codes_pass", 28, 0,),
-    ("codes_pass", 28, 1,),
-    ("shrink", 25,),
-    ("relu", 28,),
-    ("rebuild_pass", 1, 1, 0,),
-    ("rebuild_pass", 1, 1, 1,),
-    ("rebuild_pass", 1, 1, 2,),
-    ("rebuild_pass", 1, 1, 3,),
-    ("gain", 1, 0,),
-    ("codes_pass", 29, 0,),
-    ("codes_pass", 29, 1,),
-    ("interleave", 5, 3,),
-    ("interleave", 5, 2,),
-    ("shrink", 26,),
-    ("gain", 0, 0,),
-    ("cast_y", 1, 0,),
-    ("quant_h", 5,),
-    ("relu", 29,),
-    ("cast_y", 0, 0,),
-    ("rebuild_pass", 2, 0, 0,),
-    ("rebuild_pass", 2, 0, 1,),
-    ("rebuild_pass", 2, 0, 2,),
-    ("rebuild_pass", 2, 0, 3,),
-    ("codes_pass", 30, 0,),
-    ("codes_pass", 30, 1,),
-    ("shrink", 27,),
-    ("relu", 30,),
-    ("rebuild_pass", 3, 0, 0,),
-    ("rebuild_pass", 3, 0, 1,),
-    ("rebuild_pass", 3, 0, 2,),
-    ("rebuild_pass", 3, 0, 3,),
-    ("codes_pass", 31, 0,),
-    ("codes_pass", 31, 1,),
-    ("shrink", 28,),
-    ("gain", 0, 1,),
-    ("interleave", 6, 2,),
-    ("interleave", 6, 1,),
-    ("interleave", 6, 0,),
-    ("relu", 31,),
-    ("cast_y", 0, 1,),
-    ("rebuild_pass", 2, 1, 0,),
-    ("rebuild_pass", 2, 1, 1,),
-    ("rebuild_pass", 2, 1, 2,),
-    ("rebuild_pass", 2, 1, 3,),
-    ("shrink", 29,),
-    ("gain", 1, 1,),
-    ("cast_y", 1, 1,),
-    ("interleave", 6, 3,),
-    ("rebuild_pass", 3, 1, 0,),
-    ("rebuild_pass", 3, 1, 1,),
-    ("rebuild_pass", 3, 1, 2,),
-    ("rebuild_pass", 3, 1, 3,),
-    ("shrink", 30,),
-    ("quant_h", 6,),
-    ("gain", 2, 0,),
-    ("cast_y", 2, 0,),
-    ("shrink", 31,),
-    ("gain", 3, 0,),
-    ("cast_y", 3, 0,),
-    ("gain", 2, 1,),
-    ("cast_y", 2, 1,),
-    ("gain", 3, 1,),
-    ("interleave", 7, 0,),
-    ("rebuild_pass", 4, 0, 0,),
-    ("rebuild_pass", 4, 0, 1,),
-    ("rebuild_pass", 4, 0, 2,),
-    ("rebuild_pass", 5, 0, 0,),
-    ("rebuild_pass", 5, 0, 1,),
-    ("rebuild_pass", 5, 0, 2,),
-    ("rebuild_pass", 4, 1, 0,),
-    ("rebuild_pass", 4, 1, 1,),
-    ("rebuild_pass", 4, 1, 2,),
-    ("rebuild_pass", 5, 1, 0,),
-    ("rebuild_pass", 5, 1, 1,),
-    ("rebuild_pass", 5, 1, 2,),
-    ("cast_y", 3, 1,),
-    ("interleave", 7, 1,),
-    ("turn_y", 0, 2, 0,),
-    ("turn_y", 0, 2, 1,),
-    ("interleave", 7, 2,),
-    ("interleave", 7, 3,),
-    ("turn_y", 2, 2, 0,),
-    ("turn_y", 2, 2, 1,),
-    ("quant_h", 7,),
-    ("empty_y", 0, 2, 0,),
-    ("empty_y", 0, 2, 1,),
-    ("empty_y", 2, 2, 0,),
-    ("empty_y", 2, 2, 1,),
-    ("rebuild_pass", 6, 0, 0,),
-    ("rebuild_pass", 6, 0, 1,),
-    ("rebuild_pass", 6, 0, 2,),
-    ("rebuild_pass", 6, 0, 3,),
-    ("rebuild_pass", 5, 1, 3,),
-    ("rebuild_pass", 4, 1, 3,),
-    ("quant_y", 0, 2, 0,),
-    ("quant_y", 0, 2, 1,),
-    ("rebuild_pass", 5, 0, 3,),
-    ("rebuild_pass", 4, 0, 3,),
-    ("rebuild_pass", 7, 0, 0,),
-    ("rebuild_pass", 7, 0, 1,),
-    ("rebuild_pass", 7, 0, 2,),
-    ("rebuild_pass", 7, 0, 3,),
-    ("quant_y", 2, 2, 0,),
-    ("quant_y", 2, 2, 1,),
-    ("rebuild_pass", 6, 1, 0,),
-    ("rebuild_pass", 6, 1, 1,),
-    ("rebuild_pass", 6, 1, 2,),
-    ("rebuild_pass", 6, 1, 3,),
-    ("rebuild_pass", 7, 1, 0,),
-    ("rebuild_pass", 7, 1, 1,),
-    ("rebuild_pass", 7, 1, 2,),
-    ("rebuild_pass", 7, 1, 3,),
-    ("gain", 6, 0,),
-    ("gain", 5, 1,),
-    ("gain", 4, 1,),
-    ("gain", 5, 0,),
-    ("cast_y", 6, 0,),
-    ("gain", 4, 0,),
-    ("gain", 7, 0,),
-    ("cast_y", 5, 1,),
-    ("cast_y", 4, 1,),
-    ("turn_y", 4, 2, 1,),
-    ("cast_y", 5, 0,),
-    ("cast_y", 4, 0,),
-    ("turn_y", 4, 2, 0,),
-    ("cast_y", 7, 0,),
-    ("turn_y", 6, 2, 0,),
-    ("gain", 6, 1,),
-    ("cast_y", 6, 1,),
-    ("turn_y", 6, 1, 1,),
-    ("gain_bf", 7, 1,),
-    ("gain", 7, 1,),
-    ("turn_y", 7, 1, 1,),
-    ("empty_y", 4, 2, 1,),
-    ("empty_y", 4, 2, 0,),
-    ("empty_y", 6, 2, 0,),
-    ("empty_y", 6, 1, 1,),
-    ("empty_y", 7, 1, 1,),
-    ("quant_y", 4, 2, 1,),
-    ("quant_y", 4, 2, 0,),
-    ("quant_y", 6, 2, 0,),
-    ("store_scales", 0,),
-    ("quant_y", 6, 1, 1,),
-    ("quant_y", 7, 1, 1,),
+    ("order_p_scales", 0, 2),
+    ("order_p_words", 0, 0, 2),
+    ("turn_x", 0, 0),
+    ("empty_x", 0, 0, "S"),
+    ("thresholds",),
+    ("turn_x", 1, 0),
+    ("empty_x", 1, 0, "S"),
+    ("turn_x", 0, 1),
+    ("empty_x", 0, 1, "S"),
+    ("turn_x", 1, 1),
+    ("empty_x", 1, 1, "S"),
+    ("quant_x", 0, 0),
+    ("order_p_scales", 2, 2),
+    ("codes_pass", 0, 0),
+    ("codes_pass", 1, 0),
+    ("codes_pass", 2, 0),
+    ("codes_pass", 3, 0),
+    ("quant_x", 0, 1),
+    ("order_p_words", 1, 0, 2),
+    ("codes_pass", 0, 1),
+    ("codes_pass", 1, 1),
+    ("relu", 0),
+    ("order_p_words", 2, 0, 2),
+    ("codes_pass", 2, 1),
+    ("relu", 1),
+    ("turn_x", 2, 1),
+    ("turn_x", 3, 1),
+    ("empty_x", 2, 1, "S"),
+    ("codes_pass", 3, 1),
+    ("relu", 2),
+    ("shrink", 0),
+    ("codes_pass", 4, 0),
+    ("codes_pass", 4, 1),
+    ("relu", 3),
+    ("empty_x", 3, 1, "S"),
+    ("shrink", 1),
+    ("codes_pass", 5, 0),
+    ("codes_pass", 5, 1),
+    ("relu", 4),
+    ("shrink", 2),
+    ("codes_pass", 6, 0),
+    ("codes_pass", 6, 1),
+    ("relu", 5),
+    ("shrink", 3),
+    ("codes_pass", 7, 0),
+    ("codes_pass", 7, 1),
+    ("turn_x", 2, 0),
+    ("turn_x", 3, 0),
+    ("relu", 6),
+    ("empty_x", 2, 0, "S"),
+    ("order_p_words", 3, 0, 2),
+    ("shrink", 4),
+    ("codes_pass", 8, 0),
+    ("codes_pass", 8, 1),
+    ("relu", 7),
+    ("interleave", 0, 0, 1, "S"),
+    ("shrink", 5),
+    ("codes_pass", 9, 0),
+    ("codes_pass", 9, 1),
+    ("empty_x", 3, 0, "S"),
+    ("relu", 8),
+    ("shrink", 6),
+    ("codes_pass", 10, 0),
+    ("codes_pass", 10, 1),
+    ("interleave", 0, 1, 1, "G"),
+    ("interleave", 0, 2, 1, "G"),
+    ("interleave", 0, 3, 1, "G"),
+    ("relu", 9),
+    ("shrink", 7),
+    ("quant_x", 1, 1),
+    ("codes_pass", 11, 0),
+    ("codes_pass", 11, 1),
+    ("relu", 10),
+    ("quant_h", 0),
+    ("shrink", 8),
+    ("codes_pass", 12, 0),
+    ("codes_pass", 12, 1),
+    ("relu", 11),
+    ("interleave", 1, 0, 1, "S"),
+    ("shrink", 9),
+    ("codes_pass", 13, 0),
+    ("codes_pass", 13, 1),
+    ("relu", 12),
+    ("shrink", 10),
+    ("codes_pass", 14, 0),
+    ("codes_pass", 14, 1),
+    ("interleave", 1, 1, 1, "G"),
+    ("interleave", 1, 2, 1, "G"),
+    ("interleave", 1, 3, 1, "G"),
+    ("relu", 13),
+    ("shrink", 11),
+    ("quant_x", 1, 0),
+    ("codes_pass", 15, 0),
+    ("codes_pass", 15, 1),
+    ("relu", 14),
+    ("quant_h", 1),
+    ("shrink", 12),
+    ("codes_pass", 16, 0),
+    ("codes_pass", 16, 1),
+    ("relu", 15),
+    ("interleave", 2, 0, 2, "S"),
+    ("shrink", 13),
+    ("codes_pass", 17, 0),
+    ("codes_pass", 17, 1),
+    ("relu", 16),
+    ("shrink", 14),
+    ("codes_pass", 18, 0),
+    ("codes_pass", 18, 1),
+    ("interleave", 2, 2, 1, "G"),
+    ("interleave", 2, 3, 1, "G"),
+    ("relu", 17),
+    ("shrink", 15),
+    ("codes_pass", 19, 0),
+    ("codes_pass", 19, 1),
+    ("relu", 18),
+    ("quant_h", 2),
+    ("shrink", 16),
+    ("codes_pass", 20, 0),
+    ("codes_pass", 20, 1),
+    ("relu", 19),
+    ("interleave", 3, 0, 1, "S"),
+    ("shrink", 17),
+    ("codes_pass", 21, 0),
+    ("codes_pass", 21, 1),
+    ("relu", 20),
+    ("shrink", 18),
+    ("codes_pass", 22, 0),
+    ("codes_pass", 22, 1),
+    ("interleave", 3, 1, 1, "G"),
+    ("interleave", 3, 2, 1, "G"),
+    ("interleave", 3, 3, 1, "G"),
+    ("relu", 21),
+    ("shrink", 19),
+    ("codes_pass", 23, 0),
+    ("codes_pass", 23, 1),
+    ("relu", 22),
+    ("quant_h", 3),
+    ("shrink", 20),
+    ("codes_pass", 24, 0),
+    ("codes_pass", 24, 1),
+    ("relu", 23),
+    ("interleave", 4, 0, 1, "S"),
+    ("shrink", 21),
+    ("codes_pass", 25, 0),
+    ("codes_pass", 25, 1),
+    ("relu", 24),
+    ("shrink", 22),
+    ("codes_pass", 26, 0),
+    ("codes_pass", 26, 1),
+    ("interleave", 4, 1, 1, "G"),
+    ("interleave", 4, 2, 1, "G"),
+    ("interleave", 4, 3, 1, "G"),
+    ("rebuild_pass", 0, 0, 0),
+    ("rebuild_pass", 0, 0, 1),
+    ("rebuild_pass", 0, 0, 2),
+    ("rebuild_pass", 0, 0, 3),
+    ("relu", 25),
+    ("shrink", 23),
+    ("quant_h", 4),
+    ("codes_pass", 27, 0),
+    ("codes_pass", 27, 1),
+    ("relu", 26),
+    ("rebuild_pass", 1, 0, 0),
+    ("rebuild_pass", 1, 0, 1),
+    ("rebuild_pass", 1, 0, 2),
+    ("rebuild_pass", 1, 0, 3),
+    ("shrink", 24),
+    ("codes_pass", 28, 0),
+    ("codes_pass", 28, 1),
+    ("relu", 27),
+    ("interleave", 5, 0, 1, "S"),
+    ("shrink", 25),
+    ("rebuild_pass", 0, 1, 0),
+    ("rebuild_pass", 0, 1, 1),
+    ("rebuild_pass", 0, 1, 2),
+    ("rebuild_pass", 0, 1, 3),
+    ("codes_pass", 29, 0),
+    ("codes_pass", 29, 1),
+    ("relu", 28),
+    ("shrink", 26),
+    ("gain", 0, 0),
+    ("codes_pass", 30, 0),
+    ("codes_pass", 30, 1),
+    ("interleave", 5, 1, 1, "G"),
+    ("interleave", 5, 2, 1, "G"),
+    ("interleave", 5, 3, 1, "G"),
+    ("rebuild_pass", 1, 1, 0),
+    ("rebuild_pass", 1, 1, 1),
+    ("rebuild_pass", 1, 1, 2),
+    ("rebuild_pass", 1, 1, 3),
+    ("cast_y", 0, 0, 1, "S"),
+    ("relu", 29),
+    ("shrink", 27),
+    ("quant_h", 5),
+    ("codes_pass", 31, 0),
+    ("codes_pass", 31, 1),
+    ("gain", 1, 0),
+    ("relu", 30),
+    ("rebuild_pass", 2, 0, 0),
+    ("rebuild_pass", 2, 0, 1),
+    ("rebuild_pass", 2, 0, 2),
+    ("rebuild_pass", 2, 0, 3),
+    ("cast_y", 1, 0, 1, "S"),
+    ("shrink", 28),
+    ("relu", 31),
+    ("gain", 0, 1),
+    ("shrink", 29),
+    ("rebuild_pass", 3, 0, 0),
+    ("rebuild_pass", 3, 0, 1),
+    ("rebuild_pass", 3, 0, 2),
+    ("rebuild_pass", 3, 0, 3),
+    ("shrink", 30),
+    ("gain", 1, 1),
+    ("interleave", 6, 0, 1, "G"),
+    ("interleave", 6, 1, 1, "G"),
+    ("interleave", 6, 2, 1, "G"),
+    ("interleave", 6, 3, 1, "G"),
+    ("rebuild_pass", 2, 1, 0),
+    ("rebuild_pass", 2, 1, 1),
+    ("rebuild_pass", 2, 1, 2),
+    ("rebuild_pass", 2, 1, 3),
+    ("cast_y", 0, 1, 2, "S"),
+    ("shrink", 31),
+    ("quant_h", 6),
+    ("gain", 2, 0),
+    ("rebuild_pass", 3, 1, 0),
+    ("rebuild_pass", 3, 1, 1),
+    ("rebuild_pass", 3, 1, 2),
+    ("rebuild_pass", 3, 1, 3),
+    ("rebuild_pass", 4, 0, 0),
+    ("rebuild_pass", 4, 0, 1),
+    ("rebuild_pass", 4, 0, 2),
+    ("rebuild_pass", 5, 0, 0),
+    ("rebuild_pass", 5, 0, 1),
+    ("rebuild_pass", 5, 0, 2),
+    ("rebuild_pass", 4, 1, 0),
+    ("rebuild_pass", 4, 1, 1),
+    ("rebuild_pass", 4, 1, 2),
+    ("rebuild_pass", 5, 1, 0),
+    ("rebuild_pass", 5, 1, 1),
+    ("rebuild_pass", 5, 1, 2),
+    ("gain", 3, 0),
+    ("cast_y", 2, 0, 2, "S"),
+    ("gain", 2, 1),
+    ("interleave", 7, 0, 1, "G"),
+    ("interleave", 7, 1, 1, "G"),
+    ("interleave", 7, 2, 1, "G"),
+    ("interleave", 7, 3, 1, "G"),
+    ("gain", 3, 1),
+    ("cast_y", 2, 1, 2, "S"),
+    ("quant_h", 7),
+    ("turn_y", 0, 2, 0),
+    ("turn_y", 0, 2, 1),
+    ("empty_y", 0, 2, 0, "S"),
+    ("empty_y", 0, 2, 1, "S"),
+    ("turn_y", 2, 2, 0),
+    ("turn_y", 2, 2, 1),
+    ("empty_y", 2, 2, 0, "S"),
+    ("empty_y", 2, 2, 1, "S"),
+    ("quant_y", 0, 2, 0),
+    ("quant_y", 0, 2, 1),
+    ("rebuild_pass", 4, 0, 3),
+    ("rebuild_pass", 5, 0, 3),
+    ("rebuild_pass", 4, 1, 3),
+    ("rebuild_pass", 5, 1, 3),
+    ("gain", 4, 0),
+    ("rebuild_pass", 6, 0, 0),
+    ("rebuild_pass", 6, 0, 1),
+    ("rebuild_pass", 6, 0, 2),
+    ("rebuild_pass", 6, 0, 3),
+    ("gain", 5, 0),
+    ("gain", 4, 1),
+    ("gain", 5, 1),
+    ("gain", 6, 0),
+    ("rebuild_pass", 7, 0, 0),
+    ("rebuild_pass", 7, 0, 1),
+    ("rebuild_pass", 7, 0, 2),
+    ("rebuild_pass", 7, 0, 3),
+    ("quant_y", 2, 2, 0),
+    ("quant_y", 2, 2, 1),
+    ("early_scales", 512),
+    ("gain", 7, 0),
+    ("rebuild_pass", 6, 1, 0),
+    ("rebuild_pass", 6, 1, 1),
+    ("rebuild_pass", 6, 1, 2),
+    ("rebuild_pass", 6, 1, 3),
+    ("gain", 6, 1),
+    ("rebuild_pass", 7, 1, 0),
+    ("rebuild_pass", 7, 1, 1),
+    ("rebuild_pass", 7, 1, 2),
+    ("rebuild_pass", 7, 1, 3),
+    ("gain_bf", 7, 1),
+    ("gain", 7, 1),
+    ("cast_y", 4, 0, 2, "S"),
+    ("turn_y", 4, 2, 0),
+    ("cast_y", 4, 1, 2, "S"),
+    ("turn_y", 4, 2, 1),
+    ("cast_y", 6, 0, 2, "S"),
+    ("turn_y", 6, 2, 0),
+    ("cast_y", 6, 1, 1, "V"),
+    ("turn_y", 6, 1, 1),
+    ("turn_y", 7, 1, 1),
+    ("empty_y", 4, 2, 0, "S"),
+    ("empty_y", 4, 2, 1, "S"),
+    ("quant_y", 4, 2, 0),
+    ("quant_y", 4, 2, 1),
+    ("empty_y", 6, 2, 0, "S"),
+    ("quant_y", 6, 2, 0),
+    ("empty_y", 6, 1, 1, "S"),
+    ("empty_y", 7, 1, 1, "S"),
+    ("quant_y", 6, 1, 1),
+    ("quant_y", 7, 1, 1),
 ]
 
 
@@ -372,10 +355,11 @@ def tile_pinv_shrink_seismic_traces_h1_kernel(
         x_scales = tiles("x_scales", 4, [P, 512], U8)
         p_raw = tiles("p_raw", 4, [P, 2, 1024], U8)
         p_words = tiles("p_words", 4, [P, 2, 1024], U8)
-        ps_raw = sb.tile([P, 2, A], U8, name="ps_raw", align_bytes=64)
-        p_scales = tiles("p_scales", 4, [P, 2, 512], U8)
+        ps_raw = tiles("ps_raw", 2, [P, 2, 1024], U8)
+        p_scales = tiles("p_scales", 2, [P, 2, 1024], U8)
         d_words = tiles("d_words", 4, [P, 2048], U8)
         d_scales = sb.tile([P, 4, T], U8, name="d_scales", align_bytes=64)
+        lam_rows = sb.tile([P, 512], BF16, name="lam_rows", align_bytes=64)
         lam_sb = sb.tile([P, 16], BF16, name="lam_sb", align_bytes=64)
         neg_lam = sb.tile([P, 16], F32, name="neg_lam", align_bytes=64)
         tg = sb.tile([P, T], BF16, name="tg", align_bytes=64)
@@ -385,9 +369,9 @@ def tile_pinv_shrink_seismic_traces_h1_kernel(
         h_grp = tiles("h_grp", 3, [P, 2048], BF16)
         h_codes = tiles("h_codes", 8, [P, 512], U32)
         h_scales = tiles("h_scales", 8, [P, 512], U8)
-        y = tiles("y", 16, [P, 512], F32)
-        y_bf = tiles("y_bf", 16, [P, 512], BF16)
-        y_grp = tiles("y_grp", 4, [P, 1024], BF16)
+        y = tiles("y", 8, [P, 2, 512], F32)
+        y_bf = tiles("y_bf", 8, [P, 1024], BF16)
+        y_grp = tiles("y_grp", 4, [P, 2048], BF16)
         y_codes = sb.tile([P, 2, M], U32, name="y_codes", align_bytes=64)
         y_scales = sb.tile([P, 2, M], U8, name="y_scales", align_bytes=64)
 
@@ -401,6 +385,14 @@ def tile_pinv_shrink_seismic_traces_h1_kernel(
         def give(key):
             free_banks.append(held[key])
             return banks[held[key]]
+
+        def copy_on(engine, dst, src):
+            if engine == "V":
+                nc.vector.tensor_copy(out=dst, in_=src)
+            elif engine == "S":
+                nc.scalar.copy(out=dst, in_=src)
+            else:
+                nc.gpsimd.tensor_scalar(out=dst, in0=src, scalar1=1.0, scalar2=0.0, op0=ALU.mult, op1=ALU.add)
 
         def load_x(b, g):
             src = traces[256 * b : 256 * (b + 1), 512 * g : 512 * (g + 1)]
@@ -418,6 +410,18 @@ def tile_pinv_shrink_seismic_traces_h1_kernel(
         def load_d(a):
             nc.sync.dma_start(out=d_words[a][:].bitcast(I32), in_=dict_words[a].bitcast(I32))
 
+        def thresholds():
+            bank = take("lam")
+            words = lam_rows[:].bitcast(F32)
+            for u in range(2):
+                nc.tensor.transpose(bank[:, P * u : P * (u + 1)], words[:, u:256:2], ident[:])
+            give("lam")
+            nc.scalar.copy(
+                out=lam_sb[:].bitcast(F32).rearrange("p (a u) -> p a u", u=2),
+                in_=bank[:, 0 : 2 * P].rearrange("p (u r) -> p r u", u=2)[:, 0:4, :],
+            )
+            nc.scalar.activation(out=neg_lam[:], in_=lam_sb[:], func=ACT.Copy, scale=-1.0)
+
         def turn_x(b, g):
             bank = take(("x", b, g))
             words = x_raw[2 * b + g][:].rearrange("p e c -> p (e c)").bitcast(F32)
@@ -426,46 +430,45 @@ def tile_pinv_shrink_seismic_traces_h1_kernel(
                     k = 2 * e + u
                     nc.tensor.transpose(bank[:, P * k : P * (k + 1)], words[:, 256 * e + u : 256 * (e + 1) : 2], ident[:])
 
-        def empty_x(b, g):
+        def empty_x(b, g, engine):
             bank = give(("x", b, g))
             dst = x_grp[2 * (b // 2) + g][:].bitcast(F32)[:, 512 * (b % 2) : 512 * (b % 2 + 1)]
-            copy = nc.vector.tensor_copy if ("x", b, g) in EMPTY_ON_V else nc.scalar.copy
-            copy(
-                out=dst.rearrange("p (e m u) -> p e m u", e=2, u=2),
-                in_=bank[:].rearrange("p (e u m) -> p e m u", e=2, u=2),
+            copy_on(
+                engine,
+                dst.rearrange("p (e m u) -> p e m u", e=2, u=2),
+                bank[:].rearrange("p (e u m) -> p e m u", e=2, u=2),
             )
 
         def quant_x(h, g):
             k = 2 * h + g
             nc.vector.quantize_mx(out=x_codes[k][:].bitcast(FP8X4), scales=x_scales[k][:], in_=x_grp[k][:])
 
-        def order_p_words(a, g):
+        def order_p_words(a, g0, count):
             nc.vector.tensor_copy(
-                out=p_words[a][:, g, :].rearrange("p (j m e) -> p j m e", j=4, e=2),
-                in_=p_raw[a][:, g, :].rearrange("p (m j e) -> p j m e", j=4, e=2),
+                out=p_words[a][:, g0 : g0 + count, :].rearrange("p g (j m e) -> p g j m e", j=4, e=2),
+                in_=p_raw[a][:, g0 : g0 + count, :].rearrange("p g (m j e) -> p g j m e", j=4, e=2),
             )
 
-        def order_p_scales(a):
+        def order_p_scales(a, count):
+            cols = slice(512 * (a % 2), 512 * (a % 2 + count))
             nc.vector.tensor_copy(
-                out=p_scales[a][:].rearrange("p g (j m) -> p g j m", j=4),
-                in_=ps_raw[:, :, 512 * a : 512 * (a + 1)].rearrange("p g (m j) -> p g j m", j=4),
+                out=p_scales[a // 2][:, :, cols].rearrange("p g (a j m) -> p g a j m", j=4, m=P),
+                in_=ps_raw[a // 2][:, :, cols].rearrange("p g (a m j) -> p g a j m", j=4, m=P),
             )
 
         def codes_pass(s, g):
             h, a, j = s // 16, (s // 4) % 4, s % 4
             bank = take(("c", s)) if g == 0 else banks[held[("c", s)]]
+            col = 512 * (a % 2) + P * j
             nc.tensor.matmul_mx(
                 out=bank[:],
                 lhsT=p_words[a][:, g, 256 * j : 256 * (j + 1)].bitcast(FP4X4),
-                lhsT_scale=p_scales[a][:, g, P * j : P * (j + 1)],
+                lhsT_scale=p_scales[a // 2][:, g, col : col + P],
                 rhs=x_codes[2 * h + g][:].bitcast(FP8X4),
                 rhs_scale=x_scales[2 * h + g][:],
                 start=(g == 0),
                 stop=(g == 1),
             )
-
-        def neg():
-            nc.scalar.activation(out=neg_lam[:], in_=lam_sb[:], func=ACT.Copy, scale=-1.0)
 
         def relu(s):
             col = s % 16
@@ -487,17 +490,17 @@ def tile_pinv_shrink_seismic_traces_h1_kernel(
                 op1=ALU.min,
             )
 
-        def interleave(n, q):
-            dst = h_grp[n % 3][:, 512 * q : 512 * (q + 1)].rearrange("p (c i t) -> p c t i", i=4, t=4)
-            src = h_rows[n % 3][:, :, P * q : P * (q + 1)].rearrange("p t (c i) -> p c t i", i=4)
-            if ("i", n, q) in ON_G:
-                src = h_rows[n % 3][:, :, P * q : P * (q + 1)].rearrange("p t c -> p c t")
-                dst = h_grp[n % 3][:, 512 * q : 512 * (q + 1)].rearrange("p (c t) -> p c t", t=4)
-                nc.gpsimd.tensor_scalar(out=dst, in0=src, scalar1=1.0, scalar2=0.0, op0=ALU.mult, op1=ALU.add)
-            elif (n, q) in INTER_ON_V:
-                nc.vector.tensor_copy(out=dst, in_=src)
+        def interleave(n, q, count, engine):
+            dst = h_grp[n % 3][:, 512 * q : 512 * (q + count)]
+            src = h_rows[n % 3][:, :, P * q : P * (q + count)]
+            if engine == "G":
+                copy_on(engine, dst.rearrange("p (c t) -> p c t", t=4), src.rearrange("p t c -> p c t"))
             else:
-                nc.scalar.copy(out=dst, in_=src)
+                copy_on(
+                    engine,
+                    dst.rearrange("p (c i t) -> p c t i", i=4, t=4),
+                    src.rearrange("p t (c i) -> p c t i", i=4),
+                )
 
         def quant_h(n):
             nc.vector.quantize_mx(out=h_codes[n][:].bitcast(FP8X4), scales=h_scales[n][:], in_=h_grp[n % 3][:])
@@ -527,41 +530,44 @@ def tile_pinv_shrink_seismic_traces_h1_kernel(
             )
 
         def gain(i, g):
-            apply_gains(i, g, y[2 * i + g][:])
+            dst = y[2 * (i // 2) + g][:, i % 2, :]
+            apply_gains(i, g, dst)
             give(("r", i, g))
-            nc.sync.dma_start(out=out_0[P * i : P * (i + 1), 512 * g : 512 * (g + 1)], in_=y[2 * i + g][:])
+            nc.sync.dma_start(out=out_0[P * i : P * (i + 1), 512 * g : 512 * (g + 1)], in_=dst)
 
         def gain_bf(i, g):
-            apply_gains(i, g, y_bf[2 * i + g][:])
+            apply_gains(i, g, last_bf[:])
 
-        def cast_y(i, g):
-            dst = y_bf[2 * i + g][:].rearrange("p (u w e) -> p u w e", u=2, e=2)
-            src = y[2 * i + g][:].rearrange("p (w u e) -> p u w e", u=2, e=2)
-            if ("c", i, g) in ON_G:
-                nc.gpsimd.tensor_scalar(out=dst, in0=src, scalar1=1.0, scalar2=0.0, op0=ALU.mult, op1=ALU.add)
-            elif (i, g) in CAST_ON_V:
-                nc.vector.tensor_copy(out=dst, in_=src)
-            else:
-                nc.scalar.copy(out=dst, in_=src)
+        last_bf = sb.tile([P, 512], BF16, name="last_bf", align_bytes=64)
+
+        def cast_y(i, g, count, engine):
+            k = 2 * (i // 2) + g
+            cols = slice(P * (i % 2), P * (i % 2 + count))
+            dst = y_bf[k][:].rearrange("p (u w x) -> p u w x", u=2, x=2)[:, :, cols, :]
+            src = y[k][:].rearrange("p e (w u x) -> p u (e w) x", u=2, x=2)[:, :, cols, :]
+            copy_on(engine, dst, src)
 
         def turn_y(i, count, g):
             bank = take(("y", i, g))
             for e in range(count):
-                words = y_bf[2 * (i + e) + g][:].bitcast(F32)
                 for u in range(2):
                     k = 2 * e + u
-                    src = words[:, u:256:2] if (i + e, g) == (7, 1) else words[:, P * u : P * (u + 1)]
+                    if (i + e, g) == (7, 1):
+                        src = last_bf[:].bitcast(F32)[:, u:256:2]
+                    else:
+                        col = 256 * u + P * ((i + e) % 2)
+                        src = y_bf[2 * (i // 2) + g][:].bitcast(F32)[:, col : col + P]
                     nc.tensor.transpose(bank[:, P * k : P * (k + 1)], src, ident[:])
 
         def y_stage(i, count, g):
-            return y_grp[(2 * (i // 2) + g) % 4][:, 512 * (i % 2) : 512 * (i % 2 + count)]
+            return y_grp[2 * (i // 4) + g][:, 512 * (i % 4) : 512 * (i % 4 + count)]
 
-        def empty_y(i, count, g):
+        def empty_y(i, count, g, engine):
             bank = give(("y", i, g))
-            copy = nc.vector.tensor_copy if ("y", i, g) in EMPTY_ON_V else nc.scalar.copy
-            copy(
-                out=y_stage(i, count, g).bitcast(F32).rearrange("p (e m u) -> p e m u", e=count, u=2),
-                in_=bank[:, 0 : 256 * count].rearrange("p (e u m) -> p e m u", e=count, u=2),
+            copy_on(
+                engine,
+                y_stage(i, count, g).bitcast(F32).rearrange("p (e m u) -> p e m u", e=count, u=2),
+                bank[:, 0 : 256 * count].rearrange("p (e u m) -> p e m u", e=count, u=2),
             )
 
         def quant_y(i, count, g):
@@ -572,24 +578,32 @@ def tile_pinv_shrink_seismic_traces_h1_kernel(
             dst = out_1[g, :, cols, :].rearrange("p m t -> p (m t)")
             nc.sync.dma_start(out=dst.bitcast(I32), in_=y_codes[:, g, cols].bitcast(I32))
 
-        def store_scales(g):
+        def store_scales(m0, m1, queues):
             for q in range(4):
-                queue = nc.sync if (g == 0 or q < 2) else nc.scalar
-                dst = out_2[g, 4 * q : 4 * q + 4, :]
-                queue.dma_start(out=dst.bitcast(I32), in_=y_scales[32 * q : 32 * q + 4, g, :].bitcast(I32))
+                dst = out_2[:, 4 * q : 4 * q + 4, m0:m1].rearrange("g r c -> r g c")
+                queues[q % 2].dma_start(
+                    out=dst.bitcast(I32), in_=y_scales[32 * q : 32 * q + 4, :, m0:m1].bitcast(I32)
+                )
 
-        nc.vector.memset(ps_raw[:].rearrange("p g c -> p (g c)").bitcast(I32), 0)
+        def early_scales(m1):
+            store_scales(0, m1, (nc.sync, nc.sync))
+
+        def zero(engine, tile):
+            engine.memset(tile.bitcast(I32), 0)
+
+        zero(nc.vector, ps_raw[0][:].rearrange("p g c -> p (g c)"))
+        zero(nc.vector, ps_raw[1][:].rearrange("p g c -> p (g c)"))
         make_identity(nc, ident[:])
-        nc.gpsimd.memset(d_scales[:].rearrange("p g c -> p (g c)").bitcast(I32), 0)
+        nc.scalar.activation(out=lam_rows[:].bitcast(F32), in_=ps_raw[1][:, 0, :].bitcast(F32), func=ACT.Relu)
+        zero(nc.gpsimd, d_scales[:].rearrange("p g c -> p (g c)"))
         load_x(0, 0)
-        nc.sync.dma_start(
-            out=lam_sb[:].rearrange("p (a j) -> p a j", j=4), in_=lam.rearrange("(a p j) -> p a j", p=P, j=4)
-        )
-        load_scales(ps_raw, pinv_scales)
+        load_scales(ps_raw[0], pinv_scales[:, :, 0:1024])
+        nc.scalar.dma_start(out=lam_rows[0:4, :], in_=lam.rearrange("(a c) -> a c", a=4))
         load_x(1, 0)
         load_p(0)
         load_x(0, 1)
         load_x(1, 1)
+        load_scales(ps_raw[1], pinv_scales[:, :, 1024:2048])
         load_p(1)
         for g in (1, 0):
             for b in range(2, 4):
@@ -608,7 +622,7 @@ def tile_pinv_shrink_seismic_traces_h1_kernel(
             "quant_x": quant_x,
             "order_p_words": order_p_words,
             "order_p_scales": order_p_scales,
-            "neg": neg,
+            "thresholds": thresholds,
             "codes_pass": codes_pass,
             "relu": relu,
             "shrink": shrink,
@@ -621,8 +635,8 @@ def tile_pinv_shrink_seismic_traces_h1_kernel(
             "turn_y": turn_y,
             "empty_y": empty_y,
             "quant_y": quant_y,
-            "store_scales": store_scales,
+            "early_scales": early_scales,
         }
         for step in ORDER:
             table[step[0]](*step[1:])
-        store_scales(1)
+        store_scales(512, M, (nc.scalar, nc.sync))

@@ -18,318 +18,321 @@ P = 128
 FLOPS = 4 * M * T * A
 
 ORDER = [
-    ("order_p_scales", 0, 2),
+    ("thresholds",),
     ("order_p_words", 0, 0, 2),
+    ("order_p_words", 1, 0, 1),
     ("turn_x", 0, 0),
     ("empty_x", 0, 0, "S"),
-    ("thresholds",),
     ("turn_x", 1, 0),
     ("empty_x", 1, 0, "S"),
+    ("quant_x", 0, 0),
+    ("order_p_words", 1, 1, 1),
+    ("order_p_words", 2, 0, 1),
     ("turn_x", 0, 1),
     ("empty_x", 0, 1, "S"),
     ("turn_x", 1, 1),
     ("empty_x", 1, 1, "S"),
-    ("quant_x", 0, 0),
-    ("order_p_scales", 2, 2),
+    ("quant_x", 0, 1),
+    ("order_p_words", 2, 1, 1),
+    ("order_p_words", 3, 0, 2),
     ("codes_pass", 0, 0),
     ("codes_pass", 1, 0),
     ("codes_pass", 2, 0),
     ("codes_pass", 3, 0),
-    ("quant_x", 0, 1),
-    ("order_p_words", 1, 0, 2),
     ("codes_pass", 0, 1),
     ("codes_pass", 1, 1),
     ("relu", 0),
-    ("order_p_words", 2, 0, 2),
     ("codes_pass", 2, 1),
     ("relu", 1),
-    ("turn_x", 2, 1),
-    ("turn_x", 3, 1),
-    ("empty_x", 2, 1, "S"),
     ("codes_pass", 3, 1),
     ("relu", 2),
-    ("shrink", 0),
     ("codes_pass", 4, 0),
     ("codes_pass", 4, 1),
     ("relu", 3),
-    ("empty_x", 3, 1, "S"),
-    ("shrink", 1),
+    ("shrink", 0),
     ("codes_pass", 5, 0),
     ("codes_pass", 5, 1),
     ("relu", 4),
-    ("shrink", 2),
+    ("shrink", 1),
     ("codes_pass", 6, 0),
     ("codes_pass", 6, 1),
     ("relu", 5),
-    ("shrink", 3),
+    ("shrink", 2),
+    ("turn_x", 2, 1),
+    ("turn_x", 3, 1),
     ("codes_pass", 7, 0),
     ("codes_pass", 7, 1),
-    ("turn_x", 2, 0),
-    ("turn_x", 3, 0),
     ("relu", 6),
-    ("empty_x", 2, 0, "S"),
-    ("order_p_words", 3, 0, 2),
-    ("shrink", 4),
-    ("codes_pass", 8, 0),
-    ("codes_pass", 8, 1),
-    ("relu", 7),
-    ("interleave", 0, 0, 1, "S"),
-    ("shrink", 5),
-    ("codes_pass", 9, 0),
-    ("codes_pass", 9, 1),
-    ("empty_x", 3, 0, "S"),
-    ("relu", 8),
-    ("shrink", 6),
-    ("codes_pass", 10, 0),
-    ("codes_pass", 10, 1),
+    ("shrink", 3),
+    ("empty_x", 3, 1, "S"),
+    ("interleave", 0, 0, 1, "G"),
     ("interleave", 0, 1, 1, "G"),
     ("interleave", 0, 2, 1, "G"),
     ("interleave", 0, 3, 1, "G"),
+    ("codes_pass", 8, 0),
+    ("codes_pass", 8, 1),
+    ("relu", 7),
+    ("shrink", 4),
+    ("turn_x", 2, 0),
+    ("turn_x", 3, 0),
+    ("empty_x", 2, 1, "S"),
+    ("codes_pass", 9, 0),
+    ("codes_pass", 9, 1),
+    ("relu", 8),
+    ("shrink", 5),
+    ("empty_x", 3, 0, "S"),
+    ("codes_pass", 10, 0),
+    ("codes_pass", 10, 1),
     ("relu", 9),
-    ("shrink", 7),
-    ("quant_x", 1, 1),
+    ("shrink", 6),
+    ("empty_x", 2, 0, "V"),
     ("codes_pass", 11, 0),
     ("codes_pass", 11, 1),
     ("relu", 10),
-    ("quant_h", 0),
-    ("shrink", 8),
+    ("shrink", 7),
+    ("quant_x", 1, 1),
+    ("interleave", 1, 0, 2, "S"),
+    ("interleave", 1, 2, 1, "G"),
+    ("interleave", 1, 3, 1, "G"),
     ("codes_pass", 12, 0),
     ("codes_pass", 12, 1),
     ("relu", 11),
-    ("interleave", 1, 0, 1, "S"),
-    ("shrink", 9),
+    ("shrink", 8),
     ("codes_pass", 13, 0),
     ("codes_pass", 13, 1),
     ("relu", 12),
-    ("shrink", 10),
+    ("shrink", 9),
     ("codes_pass", 14, 0),
     ("codes_pass", 14, 1),
-    ("interleave", 1, 1, 1, "G"),
-    ("interleave", 1, 2, 1, "G"),
-    ("interleave", 1, 3, 1, "G"),
     ("relu", 13),
-    ("shrink", 11),
+    ("shrink", 10),
     ("quant_x", 1, 0),
+    ("quant_h", 0),
     ("codes_pass", 15, 0),
     ("codes_pass", 15, 1),
     ("relu", 14),
+    ("shrink", 11),
     ("quant_h", 1),
-    ("shrink", 12),
+    ("interleave", 2, 1, 1, "G"),
+    ("interleave", 2, 2, 1, "G"),
+    ("interleave", 2, 3, 1, "G"),
     ("codes_pass", 16, 0),
     ("codes_pass", 16, 1),
     ("relu", 15),
-    ("interleave", 2, 0, 2, "S"),
-    ("shrink", 13),
+    ("shrink", 12),
+    ("interleave", 2, 0, 1, "S"),
     ("codes_pass", 17, 0),
     ("codes_pass", 17, 1),
     ("relu", 16),
-    ("shrink", 14),
+    ("shrink", 13),
     ("codes_pass", 18, 0),
     ("codes_pass", 18, 1),
-    ("interleave", 2, 2, 1, "G"),
-    ("interleave", 2, 3, 1, "G"),
     ("relu", 17),
-    ("shrink", 15),
+    ("shrink", 14),
+    ("rebuild_pass", 0, 0, 0),
+    ("rebuild_pass", 0, 0, 1),
     ("codes_pass", 19, 0),
     ("codes_pass", 19, 1),
     ("relu", 18),
+    ("shrink", 15),
     ("quant_h", 2),
-    ("shrink", 16),
-    ("codes_pass", 20, 0),
-    ("codes_pass", 20, 1),
-    ("relu", 19),
-    ("interleave", 3, 0, 1, "S"),
-    ("shrink", 17),
-    ("codes_pass", 21, 0),
-    ("codes_pass", 21, 1),
-    ("relu", 20),
-    ("shrink", 18),
-    ("codes_pass", 22, 0),
-    ("codes_pass", 22, 1),
     ("interleave", 3, 1, 1, "G"),
     ("interleave", 3, 2, 1, "G"),
     ("interleave", 3, 3, 1, "G"),
+    ("rebuild_pass", 1, 0, 0),
+    ("rebuild_pass", 1, 0, 1),
+    ("codes_pass", 20, 0),
+    ("codes_pass", 20, 1),
+    ("relu", 19),
+    ("shrink", 16),
+    ("interleave", 3, 0, 1, "S"),
+    ("rebuild_pass", 0, 1, 0),
+    ("rebuild_pass", 0, 1, 1),
+    ("rebuild_pass", 0, 0, 2),
+    ("rebuild_pass", 1, 0, 2),
+    ("codes_pass", 21, 0),
+    ("codes_pass", 21, 1),
+    ("relu", 20),
+    ("shrink", 17),
+    ("rebuild_pass", 0, 1, 2),
+    ("codes_pass", 22, 0),
+    ("codes_pass", 22, 1),
     ("relu", 21),
-    ("shrink", 19),
+    ("shrink", 18),
     ("codes_pass", 23, 0),
     ("codes_pass", 23, 1),
     ("relu", 22),
+    ("shrink", 19),
     ("quant_h", 3),
-    ("shrink", 20),
-    ("codes_pass", 24, 0),
-    ("codes_pass", 24, 1),
-    ("relu", 23),
-    ("interleave", 4, 0, 1, "S"),
-    ("shrink", 21),
-    ("codes_pass", 25, 0),
-    ("codes_pass", 25, 1),
-    ("relu", 24),
-    ("shrink", 22),
-    ("codes_pass", 26, 0),
-    ("codes_pass", 26, 1),
+    ("interleave", 4, 0, 1, "G"),
     ("interleave", 4, 1, 1, "G"),
     ("interleave", 4, 2, 1, "G"),
     ("interleave", 4, 3, 1, "G"),
-    ("rebuild_pass", 0, 0, 0),
-    ("rebuild_pass", 0, 0, 1),
-    ("rebuild_pass", 0, 0, 2),
+    ("codes_pass", 24, 0),
+    ("codes_pass", 24, 1),
+    ("relu", 23),
+    ("shrink", 20),
     ("rebuild_pass", 0, 0, 3),
+    ("rebuild_pass", 1, 0, 3),
+    ("codes_pass", 25, 0),
+    ("codes_pass", 25, 1),
+    ("relu", 24),
+    ("shrink", 21),
+    ("rebuild_pass", 0, 1, 3),
+    ("codes_pass", 26, 0),
+    ("codes_pass", 26, 1),
     ("relu", 25),
-    ("shrink", 23),
-    ("quant_h", 4),
+    ("shrink", 22),
     ("codes_pass", 27, 0),
     ("codes_pass", 27, 1),
     ("relu", 26),
-    ("rebuild_pass", 1, 0, 0),
-    ("rebuild_pass", 1, 0, 1),
-    ("rebuild_pass", 1, 0, 2),
-    ("rebuild_pass", 1, 0, 3),
-    ("shrink", 24),
+    ("shrink", 23),
+    ("interleave", 5, 0, 2, "S"),
+    ("interleave", 5, 2, 1, "G"),
+    ("interleave", 5, 3, 1, "G"),
+    ("gain", 0, 0),
+    ("gain", 1, 0),
     ("codes_pass", 28, 0),
     ("codes_pass", 28, 1),
     ("relu", 27),
-    ("interleave", 5, 0, 1, "S"),
-    ("shrink", 25),
-    ("rebuild_pass", 0, 1, 0),
-    ("rebuild_pass", 0, 1, 1),
-    ("rebuild_pass", 0, 1, 2),
-    ("rebuild_pass", 0, 1, 3),
-    ("codes_pass", 29, 0),
-    ("codes_pass", 29, 1),
-    ("relu", 28),
-    ("shrink", 26),
-    ("gain", 0, 0),
-    ("codes_pass", 30, 0),
-    ("codes_pass", 30, 1),
-    ("interleave", 5, 1, 1, "G"),
-    ("interleave", 5, 2, 1, "G"),
-    ("interleave", 5, 3, 1, "G"),
+    ("shrink", 24),
     ("rebuild_pass", 1, 1, 0),
     ("rebuild_pass", 1, 1, 1),
     ("rebuild_pass", 1, 1, 2),
     ("rebuild_pass", 1, 1, 3),
-    ("cast_y", 0, 0, 1, "S"),
-    ("relu", 29),
-    ("shrink", 27),
-    ("quant_h", 5),
-    ("codes_pass", 31, 0),
-    ("codes_pass", 31, 1),
-    ("gain", 1, 0),
-    ("relu", 30),
+    ("codes_pass", 29, 0),
+    ("codes_pass", 29, 1),
+    ("relu", 28),
+    ("shrink", 25),
     ("rebuild_pass", 2, 0, 0),
     ("rebuild_pass", 2, 0, 1),
     ("rebuild_pass", 2, 0, 2),
     ("rebuild_pass", 2, 0, 3),
-    ("cast_y", 1, 0, 1, "S"),
-    ("shrink", 28),
+    ("cast_y", 0, 0, 1, "S"),
+    ("codes_pass", 30, 0),
+    ("codes_pass", 30, 1),
+    ("relu", 29),
+    ("shrink", 26),
+    ("quant_h", 4),
+    ("codes_pass", 31, 0),
+    ("codes_pass", 31, 1),
+    ("relu", 30),
+    ("shrink", 27),
+    ("quant_h", 5),
+    ("interleave", 6, 2, 1, "G"),
+    ("interleave", 6, 3, 1, "G"),
     ("relu", 31),
+    ("shrink", 28),
     ("gain", 0, 1),
-    ("shrink", 29),
     ("rebuild_pass", 3, 0, 0),
     ("rebuild_pass", 3, 0, 1),
     ("rebuild_pass", 3, 0, 2),
     ("rebuild_pass", 3, 0, 3),
-    ("shrink", 30),
-    ("gain", 1, 1),
-    ("interleave", 6, 0, 1, "G"),
-    ("interleave", 6, 1, 1, "G"),
-    ("interleave", 6, 2, 1, "G"),
-    ("interleave", 6, 3, 1, "G"),
+    ("cast_y", 1, 0, 1, "G"),
+    ("shrink", 29),
     ("rebuild_pass", 2, 1, 0),
     ("rebuild_pass", 2, 1, 1),
     ("rebuild_pass", 2, 1, 2),
     ("rebuild_pass", 2, 1, 3),
-    ("cast_y", 0, 1, 2, "S"),
+    ("shrink", 30),
+    ("interleave", 6, 0, 2, "S"),
     ("shrink", 31),
     ("quant_h", 6),
-    ("gain", 2, 0),
+    ("gain", 1, 1),
     ("rebuild_pass", 3, 1, 0),
     ("rebuild_pass", 3, 1, 1),
     ("rebuild_pass", 3, 1, 2),
     ("rebuild_pass", 3, 1, 3),
+    ("cast_y", 0, 1, 1, "S"),
     ("rebuild_pass", 4, 0, 0),
     ("rebuild_pass", 4, 0, 1),
-    ("rebuild_pass", 4, 0, 2),
     ("rebuild_pass", 5, 0, 0),
     ("rebuild_pass", 5, 0, 1),
-    ("rebuild_pass", 5, 0, 2),
     ("rebuild_pass", 4, 1, 0),
     ("rebuild_pass", 4, 1, 1),
-    ("rebuild_pass", 4, 1, 2),
     ("rebuild_pass", 5, 1, 0),
     ("rebuild_pass", 5, 1, 1),
-    ("rebuild_pass", 5, 1, 2),
-    ("gain", 3, 0),
-    ("cast_y", 2, 0, 2, "S"),
-    ("gain", 2, 1),
-    ("interleave", 7, 0, 1, "G"),
-    ("interleave", 7, 1, 1, "G"),
+    ("interleave", 7, 0, 2, "S"),
     ("interleave", 7, 2, 1, "G"),
     ("interleave", 7, 3, 1, "G"),
+    ("gain", 2, 0),
+    ("gain", 3, 0),
+    ("gain", 2, 1),
     ("gain", 3, 1),
-    ("cast_y", 2, 1, 2, "S"),
+    ("cast_y", 1, 1, 1, "S"),
+    ("cast_y", 2, 0, 1, "G"),
+    ("cast_y", 3, 0, 1, "S"),
+    ("cast_y", 2, 1, 1, "S"),
+    ("cast_y", 3, 1, 1, "V"),
+    ("rebuild_pass", 4, 0, 2),
+    ("rebuild_pass", 5, 0, 2),
+    ("rebuild_pass", 4, 1, 2),
+    ("rebuild_pass", 5, 1, 2),
     ("quant_h", 7),
     ("turn_y", 0, 2, 0),
     ("turn_y", 0, 2, 1),
-    ("empty_y", 0, 2, 0, "S"),
-    ("empty_y", 0, 2, 1, "S"),
     ("turn_y", 2, 2, 0),
     ("turn_y", 2, 2, 1),
+    ("empty_y", 0, 2, 0, "S"),
+    ("empty_y", 0, 2, 1, "S"),
     ("empty_y", 2, 2, 0, "S"),
     ("empty_y", 2, 2, 1, "S"),
-    ("quant_y", 0, 2, 0),
-    ("quant_y", 0, 2, 1),
     ("rebuild_pass", 4, 0, 3),
     ("rebuild_pass", 5, 0, 3),
     ("rebuild_pass", 4, 1, 3),
     ("rebuild_pass", 5, 1, 3),
+    ("quant_y", 0, 2, 0),
     ("gain", 4, 0),
+    ("quant_y", 0, 2, 1),
+    ("gain", 5, 0),
+    ("quant_y", 2, 2, 0),
+    ("gain", 4, 1),
+    ("gain", 5, 1),
+    ("cast_y", 4, 0, 1, "S"),
+    ("cast_y", 5, 0, 1, "G"),
+    ("cast_y", 4, 1, 1, "S"),
+    ("cast_y", 5, 1, 1, "S"),
     ("rebuild_pass", 6, 0, 0),
     ("rebuild_pass", 6, 0, 1),
     ("rebuild_pass", 6, 0, 2),
     ("rebuild_pass", 6, 0, 3),
-    ("gain", 5, 0),
-    ("gain", 4, 1),
-    ("gain", 5, 1),
-    ("gain", 6, 0),
     ("rebuild_pass", 7, 0, 0),
     ("rebuild_pass", 7, 0, 1),
     ("rebuild_pass", 7, 0, 2),
     ("rebuild_pass", 7, 0, 3),
-    ("quant_y", 2, 2, 0),
+    ("gain", 6, 0),
     ("quant_y", 2, 2, 1),
     ("early_scales", 512),
+    ("cast_y", 6, 0, 1, "V"),
     ("gain", 7, 0),
     ("rebuild_pass", 6, 1, 0),
     ("rebuild_pass", 6, 1, 1),
     ("rebuild_pass", 6, 1, 2),
     ("rebuild_pass", 6, 1, 3),
-    ("gain", 6, 1),
     ("rebuild_pass", 7, 1, 0),
     ("rebuild_pass", 7, 1, 1),
     ("rebuild_pass", 7, 1, 2),
     ("rebuild_pass", 7, 1, 3),
+    ("gain", 6, 1),
+    ("cast_y", 7, 0, 1, "G"),
+    ("cast_y", 6, 1, 1, "G"),
+    ("turn_y", 4, 2, 0),
+    ("turn_y", 4, 2, 1),
     ("gain_bf", 7, 1),
     ("gain", 7, 1),
-    ("cast_y", 4, 0, 2, "S"),
-    ("turn_y", 4, 2, 0),
-    ("cast_y", 4, 1, 2, "S"),
-    ("turn_y", 4, 2, 1),
-    ("cast_y", 6, 0, 2, "S"),
-    ("turn_y", 6, 2, 0),
-    ("cast_y", 6, 1, 1, "V"),
-    ("turn_y", 6, 1, 1),
     ("turn_y", 7, 1, 1),
+    ("turn_y", 6, 2, 0),
+    ("turn_y", 6, 1, 1),
     ("empty_y", 4, 2, 0, "S"),
     ("empty_y", 4, 2, 1, "S"),
+    ("empty_y", 7, 1, 1, "S"),
+    ("empty_y", 6, 2, 0, "S"),
+    ("empty_y", 6, 1, 1, "S"),
     ("quant_y", 4, 2, 0),
     ("quant_y", 4, 2, 1),
-    ("empty_y", 6, 2, 0, "S"),
-    ("quant_y", 6, 2, 0),
-    ("empty_y", 6, 1, 1, "S"),
-    ("empty_y", 7, 1, 1, "S"),
-    ("quant_y", 6, 1, 1),
     ("quant_y", 7, 1, 1),
+    ("quant_y", 6, 2, 0),
+    ("quant_y", 6, 1, 1),
 ]
 
 
@@ -355,12 +358,12 @@ def tile_pinv_shrink_seismic_traces_h1_kernel(
         x_scales = tiles("x_scales", 4, [P, 512], U8)
         p_raw = tiles("p_raw", 4, [P, 2, 1024], U8)
         p_words = tiles("p_words", 4, [P, 2, 1024], U8)
-        ps_raw = tiles("ps_raw", 2, [P, 2, 1024], U8)
-        p_scales = tiles("p_scales", 2, [P, 2, 1024], U8)
+        ps_raw = sb.tile([P, A], U8, name="ps_raw", align_bytes=64)
+        ps_ord = sb.tile([P, A], U8, name="ps_ord", align_bytes=64)
+        p_scales = sb.tile([P, 2, A], U8, name="p_scales", align_bytes=64)
         d_words = tiles("d_words", 4, [P, 2048], U8)
         d_scales = sb.tile([P, 4, T], U8, name="d_scales", align_bytes=64)
         lam_rows = sb.tile([P, 512], BF16, name="lam_rows", align_bytes=64)
-        lam_sb = sb.tile([P, 16], BF16, name="lam_sb", align_bytes=64)
         neg_lam = sb.tile([P, 16], F32, name="neg_lam", align_bytes=64)
         tg = sb.tile([P, T], BF16, name="tg", align_bytes=64)
         trg = sb.tile([P, 8, 2], BF16, name="trg", align_bytes=64)
@@ -369,11 +372,11 @@ def tile_pinv_shrink_seismic_traces_h1_kernel(
         h_grp = tiles("h_grp", 3, [P, 2048], BF16)
         h_codes = tiles("h_codes", 8, [P, 512], U32)
         h_scales = tiles("h_scales", 8, [P, 512], U8)
-        y = tiles("y", 8, [P, 2, 512], F32)
-        y_bf = tiles("y_bf", 8, [P, 1024], BF16)
+        y = tiles("y", 16, [P, 512], F32)
+        y_bf = tiles("y_bf", 15, [P, 512], BF16)
         y_grp = tiles("y_grp", 4, [P, 2048], BF16)
         y_codes = sb.tile([P, 2, M], U32, name="y_codes", align_bytes=64)
-        y_scales = sb.tile([P, 2, M], U8, name="y_scales", align_bytes=64)
+        y_scales = tiles("y_scales", 2, [P, 2, 512], U8)
 
         held = {}
 
@@ -416,11 +419,12 @@ def tile_pinv_shrink_seismic_traces_h1_kernel(
             for u in range(2):
                 nc.tensor.transpose(bank[:, P * u : P * (u + 1)], words[:, u:256:2], ident[:])
             give("lam")
-            nc.scalar.copy(
-                out=lam_sb[:].bitcast(F32).rearrange("p (a u) -> p a u", u=2),
-                in_=bank[:, 0 : 2 * P].rearrange("p (u r) -> p r u", u=2)[:, 0:4, :],
+            nc.scalar.activation(
+                out=neg_lam[:].rearrange("p (a u e) -> p a u e", u=2, e=2),
+                in_=bank[:, 0 : 2 * P].bitcast(BF16).rearrange("p (u r e) -> p r u e", u=2, e=2)[:, 0:4, :, :],
+                func=ACT.Copy,
+                scale=-1.0,
             )
-            nc.scalar.activation(out=neg_lam[:], in_=lam_sb[:], func=ACT.Copy, scale=-1.0)
 
         def turn_x(b, g):
             bank = take(("x", b, g))
@@ -450,20 +454,27 @@ def tile_pinv_shrink_seismic_traces_h1_kernel(
             )
 
         def order_p_scales(a, count):
-            cols = slice(512 * (a % 2), 512 * (a % 2 + count))
             nc.vector.tensor_copy(
-                out=p_scales[a // 2][:, :, cols].rearrange("p g (a j m) -> p g a j m", j=4, m=P),
-                in_=ps_raw[a // 2][:, :, cols].rearrange("p g (a m j) -> p g a j m", j=4, m=P),
+                out=ps_ord[:].rearrange("p (a j m) -> p a j m", j=4, m=P),
+                in_=ps_raw[:].rearrange("p (a m j) -> p a j m", j=4, m=P),
             )
+
+        def spread_p_scales():
+            for g in range(2):
+                for q in range(4):
+                    row = 16 * g + 4 * q
+                    nc.sync.dma_start(
+                        out=p_scales[32 * q : 32 * q + 4, g, :].bitcast(I32), in_=ps_ord[row : row + 4, :].bitcast(I32)
+                    )
 
         def codes_pass(s, g):
             h, a, j = s // 16, (s // 4) % 4, s % 4
             bank = take(("c", s)) if g == 0 else banks[held[("c", s)]]
-            col = 512 * (a % 2) + P * j
+            col = 512 * a + P * j
             nc.tensor.matmul_mx(
                 out=bank[:],
                 lhsT=p_words[a][:, g, 256 * j : 256 * (j + 1)].bitcast(FP4X4),
-                lhsT_scale=p_scales[a // 2][:, g, col : col + P],
+                lhsT_scale=p_scales[:, g, col : col + P],
                 rhs=x_codes[2 * h + g][:].bitcast(FP8X4),
                 rhs_scale=x_scales[2 * h + g][:],
                 start=(g == 0),
@@ -484,9 +495,9 @@ def tile_pinv_shrink_seismic_traces_h1_kernel(
             nc.vector.scalar_tensor_tensor(
                 out=h_rows[n % 3][:, j, :],
                 in0=bank[:],
-                scalar=lam_sb[:, col : col + 1],
+                scalar=neg_lam[:, col : col + 1],
                 in1=upper[s % 4][:],
-                op0=ALU.add,
+                op0=ALU.subtract,
                 op1=ALU.min,
             )
 
@@ -530,7 +541,7 @@ def tile_pinv_shrink_seismic_traces_h1_kernel(
             )
 
         def gain(i, g):
-            dst = y[2 * (i // 2) + g][:, i % 2, :]
+            dst = y[2 * i + g][:]
             apply_gains(i, g, dst)
             give(("r", i, g))
             nc.sync.dma_start(out=out_0[P * i : P * (i + 1), 512 * g : 512 * (g + 1)], in_=dst)
@@ -541,10 +552,8 @@ def tile_pinv_shrink_seismic_traces_h1_kernel(
         last_bf = sb.tile([P, 512], BF16, name="last_bf", align_bytes=64)
 
         def cast_y(i, g, count, engine):
-            k = 2 * (i // 2) + g
-            cols = slice(P * (i % 2), P * (i % 2 + count))
-            dst = y_bf[k][:].rearrange("p (u w x) -> p u w x", u=2, x=2)[:, :, cols, :]
-            src = y[k][:].rearrange("p e (w u x) -> p u (e w) x", u=2, x=2)[:, :, cols, :]
+            dst = y_bf[2 * i + g][:].rearrange("p (u w x) -> p u w x", u=2, x=2)
+            src = y[2 * i + g][:].rearrange("p (w u x) -> p u w x", u=2, x=2)
             copy_on(engine, dst, src)
 
         def turn_y(i, count, g):
@@ -555,8 +564,7 @@ def tile_pinv_shrink_seismic_traces_h1_kernel(
                     if (i + e, g) == (7, 1):
                         src = last_bf[:].bitcast(F32)[:, u:256:2]
                     else:
-                        col = 256 * u + P * ((i + e) % 2)
-                        src = y_bf[2 * (i // 2) + g][:].bitcast(F32)[:, col : col + P]
+                        src = y_bf[2 * (i + e) + g][:].bitcast(F32)[:, P * u : P * (u + 1)]
                     nc.tensor.transpose(bank[:, P * k : P * (k + 1)], src, ident[:])
 
         def y_stage(i, count, g):
@@ -573,7 +581,7 @@ def tile_pinv_shrink_seismic_traces_h1_kernel(
         def quant_y(i, count, g):
             cols = slice(P * i, P * (i + count))
             nc.vector.quantize_mx(
-                out=y_codes[:, g, cols].bitcast(FP8X4), scales=y_scales[:, g, cols], in_=y_stage(i, count, g)
+                out=y_codes[:, g, cols].bitcast(FP8X4), scales=y_scales[i // 4][:, g, P * (i % 4) : P * (i % 4 + count)], in_=y_stage(i, count, g)
             )
             dst = out_1[g, :, cols, :].rearrange("p m t -> p (m t)")
             nc.sync.dma_start(out=dst.bitcast(I32), in_=y_codes[:, g, cols].bitcast(I32))
@@ -582,33 +590,39 @@ def tile_pinv_shrink_seismic_traces_h1_kernel(
             for q in range(4):
                 dst = out_2[:, 4 * q : 4 * q + 4, m0:m1].rearrange("g r c -> r g c")
                 queues[q % 2].dma_start(
-                    out=dst.bitcast(I32), in_=y_scales[32 * q : 32 * q + 4, :, m0:m1].bitcast(I32)
+                    out=dst.bitcast(I32), in_=y_scales[m0 // 512][32 * q : 32 * q + 4, :, :].bitcast(I32)
                 )
 
         def early_scales(m1):
             store_scales(0, m1, (nc.sync, nc.sync))
 
+        def zero_d():
+            zero(nc.vector, d_scales[:].rearrange("p g c -> p (g c)"))
+
         def zero(engine, tile):
             engine.memset(tile.bitcast(I32), 0)
 
-        zero(nc.vector, ps_raw[0][:].rearrange("p g c -> p (g c)"))
-        zero(nc.vector, ps_raw[1][:].rearrange("p g c -> p (g c)"))
         make_identity(nc, ident[:])
-        nc.scalar.activation(out=lam_rows[:].bitcast(F32), in_=ps_raw[1][:, 0, :].bitcast(F32), func=ACT.Relu)
-        zero(nc.gpsimd, d_scales[:].rearrange("p g c -> p (g c)"))
-        load_x(0, 0)
-        load_scales(ps_raw[0], pinv_scales[:, :, 0:1024])
+        zero(nc.vector, lam_rows[:])
+        zero(nc.vector, ps_raw[:])
+        zero(nc.vector, p_scales[:].rearrange("p g c -> p (g c)"))
+        zero_d()
         nc.scalar.dma_start(out=lam_rows[0:4, :], in_=lam.rearrange("(a c) -> a c", a=4))
-        load_x(1, 0)
+        load_x(0, 0)
+        nc.sync.dma_start(out=ps_raw[0:32, :].bitcast(I32), in_=pinv_scales.rearrange("g q c -> (g q) c").bitcast(I32))
+        order_p_scales(0, 1)
         load_p(0)
+        load_x(1, 0)
+        load_p(1)
         load_x(0, 1)
         load_x(1, 1)
-        load_scales(ps_raw[1], pinv_scales[:, :, 1024:2048])
-        load_p(1)
-        for g in (1, 0):
+        spread_p_scales()
+        load_p(2)
+        for g in range(2):
             for b in range(2, 4):
                 load_x(b, g)
-            load_p(3 - g)
+            if g == 0:
+                load_p(3)
         load_scales(d_scales, dict_scales)
         for a in range(4):
             load_d(a)

@@ -14,326 +14,20 @@ ALU = mybir.AluOpType
 ACT = mybir.ActivationFunctionType
 
 M, T, A = 1024, 1024, 2048
-P = 128
 FLOPS = 4 * M * T * A
 
-ORDER = [
-    ("thresholds",),
-    ("order_p_words", 0, 0, 2),
-    ("order_p_words", 1, 0, 1),
-    ("turn_x", 0, 0),
-    ("empty_x", 0, 0, "S"),
-    ("turn_x", 1, 0),
-    ("empty_x", 1, 0, "S"),
-    ("quant_x", 0, 0),
-    ("order_p_words", 1, 1, 1),
-    ("order_p_words", 2, 0, 1),
-    ("turn_x", 0, 1),
-    ("empty_x", 0, 1, "S"),
-    ("turn_x", 1, 1),
-    ("empty_x", 1, 1, "S"),
-    ("quant_x", 0, 1),
-    ("order_p_words", 2, 1, 1),
-    ("order_p_words", 3, 0, 2),
-    ("codes_pass", 0, 0),
-    ("codes_pass", 1, 0),
-    ("codes_pass", 2, 0),
-    ("codes_pass", 3, 0),
-    ("codes_pass", 0, 1),
-    ("codes_pass", 1, 1),
-    ("relu", 0),
-    ("codes_pass", 2, 1),
-    ("relu", 1),
-    ("codes_pass", 3, 1),
-    ("relu", 2),
-    ("codes_pass", 4, 0),
-    ("codes_pass", 4, 1),
-    ("relu", 3),
-    ("shrink", 0),
-    ("codes_pass", 5, 0),
-    ("codes_pass", 5, 1),
-    ("relu", 4),
-    ("shrink", 1),
-    ("codes_pass", 6, 0),
-    ("codes_pass", 6, 1),
-    ("relu", 5),
-    ("shrink", 2),
-    ("turn_x", 2, 1),
-    ("turn_x", 3, 1),
-    ("codes_pass", 7, 0),
-    ("codes_pass", 7, 1),
-    ("relu", 6),
-    ("shrink", 3),
-    ("empty_x", 3, 1, "S"),
-    ("interleave", 0, 0, 1, "G"),
-    ("interleave", 0, 1, 1, "G"),
-    ("interleave", 0, 2, 1, "G"),
-    ("interleave", 0, 3, 1, "G"),
-    ("codes_pass", 8, 0),
-    ("codes_pass", 8, 1),
-    ("relu", 7),
-    ("shrink", 4),
-    ("turn_x", 2, 0),
-    ("turn_x", 3, 0),
-    ("empty_x", 2, 1, "S"),
-    ("codes_pass", 9, 0),
-    ("codes_pass", 9, 1),
-    ("relu", 8),
-    ("shrink", 5),
-    ("empty_x", 3, 0, "S"),
-    ("codes_pass", 10, 0),
-    ("codes_pass", 10, 1),
-    ("relu", 9),
-    ("shrink", 6),
-    ("empty_x", 2, 0, "V"),
-    ("codes_pass", 11, 0),
-    ("codes_pass", 11, 1),
-    ("relu", 10),
-    ("shrink", 7),
-    ("quant_x", 1, 1),
-    ("interleave", 1, 0, 2, "S"),
-    ("interleave", 1, 2, 1, "G"),
-    ("interleave", 1, 3, 1, "G"),
-    ("codes_pass", 12, 0),
-    ("codes_pass", 12, 1),
-    ("relu", 11),
-    ("shrink", 8),
-    ("codes_pass", 13, 0),
-    ("codes_pass", 13, 1),
-    ("relu", 12),
-    ("shrink", 9),
-    ("codes_pass", 14, 0),
-    ("codes_pass", 14, 1),
-    ("relu", 13),
-    ("shrink", 10),
-    ("quant_x", 1, 0),
-    ("quant_h", 0),
-    ("codes_pass", 15, 0),
-    ("codes_pass", 15, 1),
-    ("relu", 14),
-    ("shrink", 11),
-    ("quant_h", 1),
-    ("interleave", 2, 1, 1, "G"),
-    ("interleave", 2, 2, 1, "G"),
-    ("interleave", 2, 3, 1, "G"),
-    ("codes_pass", 16, 0),
-    ("codes_pass", 16, 1),
-    ("relu", 15),
-    ("shrink", 12),
-    ("interleave", 2, 0, 1, "S"),
-    ("codes_pass", 17, 0),
-    ("codes_pass", 17, 1),
-    ("relu", 16),
-    ("shrink", 13),
-    ("codes_pass", 18, 0),
-    ("codes_pass", 18, 1),
-    ("relu", 17),
-    ("shrink", 14),
-    ("rebuild_pass", 0, 0, 0),
-    ("rebuild_pass", 0, 0, 1),
-    ("codes_pass", 19, 0),
-    ("codes_pass", 19, 1),
-    ("relu", 18),
-    ("shrink", 15),
-    ("quant_h", 2),
-    ("interleave", 3, 1, 1, "G"),
-    ("interleave", 3, 2, 1, "G"),
-    ("interleave", 3, 3, 1, "G"),
-    ("rebuild_pass", 1, 0, 0),
-    ("rebuild_pass", 1, 0, 1),
-    ("codes_pass", 20, 0),
-    ("codes_pass", 20, 1),
-    ("relu", 19),
-    ("shrink", 16),
-    ("interleave", 3, 0, 1, "S"),
-    ("rebuild_pass", 0, 1, 0),
-    ("rebuild_pass", 0, 1, 1),
-    ("rebuild_pass", 0, 0, 2),
-    ("rebuild_pass", 1, 0, 2),
-    ("codes_pass", 21, 0),
-    ("codes_pass", 21, 1),
-    ("relu", 20),
-    ("shrink", 17),
-    ("rebuild_pass", 0, 1, 2),
-    ("codes_pass", 22, 0),
-    ("codes_pass", 22, 1),
-    ("relu", 21),
-    ("shrink", 18),
-    ("codes_pass", 23, 0),
-    ("codes_pass", 23, 1),
-    ("relu", 22),
-    ("shrink", 19),
-    ("quant_h", 3),
-    ("interleave", 4, 0, 1, "G"),
-    ("interleave", 4, 1, 1, "G"),
-    ("interleave", 4, 2, 1, "G"),
-    ("interleave", 4, 3, 1, "G"),
-    ("codes_pass", 24, 0),
-    ("codes_pass", 24, 1),
-    ("relu", 23),
-    ("shrink", 20),
-    ("rebuild_pass", 0, 0, 3),
-    ("rebuild_pass", 1, 0, 3),
-    ("codes_pass", 25, 0),
-    ("codes_pass", 25, 1),
-    ("relu", 24),
-    ("shrink", 21),
-    ("rebuild_pass", 0, 1, 3),
-    ("codes_pass", 26, 0),
-    ("codes_pass", 26, 1),
-    ("relu", 25),
-    ("shrink", 22),
-    ("codes_pass", 27, 0),
-    ("codes_pass", 27, 1),
-    ("relu", 26),
-    ("shrink", 23),
-    ("interleave", 5, 0, 2, "S"),
-    ("interleave", 5, 2, 1, "G"),
-    ("interleave", 5, 3, 1, "G"),
-    ("gain", 0, 0),
-    ("gain", 1, 0),
-    ("codes_pass", 28, 0),
-    ("codes_pass", 28, 1),
-    ("relu", 27),
-    ("shrink", 24),
-    ("rebuild_pass", 1, 1, 0),
-    ("rebuild_pass", 1, 1, 1),
-    ("rebuild_pass", 1, 1, 2),
-    ("rebuild_pass", 1, 1, 3),
-    ("codes_pass", 29, 0),
-    ("codes_pass", 29, 1),
-    ("relu", 28),
-    ("shrink", 25),
-    ("rebuild_pass", 2, 0, 0),
-    ("rebuild_pass", 2, 0, 1),
-    ("rebuild_pass", 2, 0, 2),
-    ("rebuild_pass", 2, 0, 3),
-    ("cast_y", 0, 0, 1, "S"),
-    ("codes_pass", 30, 0),
-    ("codes_pass", 30, 1),
-    ("relu", 29),
-    ("shrink", 26),
-    ("quant_h", 4),
-    ("codes_pass", 31, 0),
-    ("codes_pass", 31, 1),
-    ("relu", 30),
-    ("shrink", 27),
-    ("quant_h", 5),
-    ("interleave", 6, 2, 1, "G"),
-    ("interleave", 6, 3, 1, "G"),
-    ("relu", 31),
-    ("shrink", 28),
-    ("gain", 0, 1),
-    ("rebuild_pass", 3, 0, 0),
-    ("rebuild_pass", 3, 0, 1),
-    ("rebuild_pass", 3, 0, 2),
-    ("rebuild_pass", 3, 0, 3),
-    ("cast_y", 1, 0, 1, "G"),
-    ("shrink", 29),
-    ("rebuild_pass", 2, 1, 0),
-    ("rebuild_pass", 2, 1, 1),
-    ("rebuild_pass", 2, 1, 2),
-    ("rebuild_pass", 2, 1, 3),
-    ("shrink", 30),
-    ("interleave", 6, 0, 2, "S"),
-    ("shrink", 31),
-    ("quant_h", 6),
-    ("gain", 1, 1),
-    ("rebuild_pass", 3, 1, 0),
-    ("rebuild_pass", 3, 1, 1),
-    ("rebuild_pass", 3, 1, 2),
-    ("rebuild_pass", 3, 1, 3),
-    ("cast_y", 0, 1, 1, "S"),
-    ("rebuild_pass", 4, 0, 0),
-    ("rebuild_pass", 4, 0, 1),
-    ("rebuild_pass", 5, 0, 0),
-    ("rebuild_pass", 5, 0, 1),
-    ("rebuild_pass", 4, 1, 0),
-    ("rebuild_pass", 4, 1, 1),
-    ("rebuild_pass", 5, 1, 0),
-    ("rebuild_pass", 5, 1, 1),
-    ("interleave", 7, 0, 2, "S"),
-    ("interleave", 7, 2, 1, "G"),
-    ("interleave", 7, 3, 1, "G"),
-    ("gain", 2, 0),
-    ("gain", 3, 0),
-    ("gain", 2, 1),
-    ("gain", 3, 1),
-    ("cast_y", 1, 1, 1, "S"),
-    ("cast_y", 2, 0, 1, "G"),
-    ("cast_y", 3, 0, 1, "S"),
-    ("cast_y", 2, 1, 1, "S"),
-    ("cast_y", 3, 1, 1, "V"),
-    ("rebuild_pass", 4, 0, 2),
-    ("rebuild_pass", 5, 0, 2),
-    ("rebuild_pass", 4, 1, 2),
-    ("rebuild_pass", 5, 1, 2),
-    ("quant_h", 7),
-    ("turn_y", 0, 2, 0),
-    ("turn_y", 0, 2, 1),
-    ("turn_y", 2, 2, 0),
-    ("turn_y", 2, 2, 1),
-    ("empty_y", 0, 2, 0, "S"),
-    ("empty_y", 0, 2, 1, "S"),
-    ("empty_y", 2, 2, 0, "S"),
-    ("empty_y", 2, 2, 1, "S"),
-    ("rebuild_pass", 4, 0, 3),
-    ("rebuild_pass", 5, 0, 3),
-    ("rebuild_pass", 4, 1, 3),
-    ("rebuild_pass", 5, 1, 3),
-    ("quant_y", 0, 2, 0),
-    ("gain", 4, 0),
-    ("quant_y", 0, 2, 1),
-    ("gain", 5, 0),
-    ("quant_y", 2, 2, 0),
-    ("gain", 4, 1),
-    ("gain", 5, 1),
-    ("cast_y", 4, 0, 1, "S"),
-    ("cast_y", 5, 0, 1, "G"),
-    ("cast_y", 4, 1, 1, "S"),
-    ("cast_y", 5, 1, 1, "S"),
-    ("rebuild_pass", 6, 0, 0),
-    ("rebuild_pass", 6, 0, 1),
-    ("rebuild_pass", 6, 0, 2),
-    ("rebuild_pass", 6, 0, 3),
-    ("rebuild_pass", 7, 0, 0),
-    ("rebuild_pass", 7, 0, 1),
-    ("rebuild_pass", 7, 0, 2),
-    ("rebuild_pass", 7, 0, 3),
-    ("gain", 6, 0),
-    ("quant_y", 2, 2, 1),
-    ("early_scales", 512),
-    ("cast_y", 6, 0, 1, "V"),
-    ("gain", 7, 0),
-    ("rebuild_pass", 6, 1, 0),
-    ("rebuild_pass", 6, 1, 1),
-    ("rebuild_pass", 6, 1, 2),
-    ("rebuild_pass", 6, 1, 3),
-    ("rebuild_pass", 7, 1, 0),
-    ("rebuild_pass", 7, 1, 1),
-    ("rebuild_pass", 7, 1, 2),
-    ("rebuild_pass", 7, 1, 3),
-    ("gain", 6, 1),
-    ("cast_y", 7, 0, 1, "G"),
-    ("cast_y", 6, 1, 1, "G"),
-    ("turn_y", 4, 2, 0),
-    ("turn_y", 4, 2, 1),
-    ("gain_bf", 7, 1),
-    ("gain", 7, 1),
-    ("turn_y", 7, 1, 1),
-    ("turn_y", 6, 2, 0),
-    ("turn_y", 6, 1, 1),
-    ("empty_y", 4, 2, 0, "S"),
-    ("empty_y", 4, 2, 1, "S"),
-    ("empty_y", 7, 1, 1, "S"),
-    ("empty_y", 6, 2, 0, "S"),
-    ("empty_y", 6, 1, 1, "S"),
-    ("quant_y", 4, 2, 0),
-    ("quant_y", 4, 2, 1),
-    ("quant_y", 7, 1, 1),
-    ("quant_y", 6, 2, 0),
-    ("quant_y", 6, 1, 1),
-]
+P = 128
+N = 512
+SLOTS = 32
+PSUM_BANKS = 8
+UPPER_BUFS = 4
+UNIT_BUFS = 3
+CODES_AHEAD = 4
+RELU_AHEAD = 3
+QUARTERS_ON_SCALAR = (0, 2, 2, 1, 0, 3, 1, 2)
+SCALAR_QUARTERS_AFTER = (3, 5, 4, 4, 3, 3, 3)
+QUANT_H_AFTER = (10, 11, 15, 19, 25, 27, 31)
+LAST = (7, 1)
 
 
 def tile_pinv_shrink_seismic_traces_h1_kernel(
@@ -345,80 +39,108 @@ def tile_pinv_shrink_seismic_traces_h1_kernel(
         pp = ctx.enter_context(tc.psum_pool(name="pp", bufs=1))
         ctx.enter_context(tc.manual_schedule())
 
+        def one_tile(name, shape, dtype):
+            return sb.tile(shape, dtype, name=name, align_bytes=64)
+
         def tiles(name, count, shape, dtype):
-            return [sb.tile(shape, dtype, name="%s%d" % (name, k), align_bytes=64) for k in range(count)]
+            return [one_tile("%s%d" % (name, k), shape, dtype) for k in range(count)]
 
-        banks = [pp.tile([P, 512], F32, name="bank%d" % k) for k in range(8)]
-        free_banks = list(range(8))
+        banks = [pp.tile([P, N], F32, name="bank%d" % k) for k in range(PSUM_BANKS)]
+        ident = one_tile("ident", [P, P], F32)
+        x_raw = tiles("x_raw", 8, [P, 2, N], BF16)
+        x_words = tiles("x_words", 4, [P, 4 * N], BF16)
+        x_codes = tiles("x_codes", 4, [P, N], U32)
+        x_scales = tiles("x_scales", 4, [P, N], U8)
+        p_raw = tiles("p_raw", 4, [P, 2, 2 * N], U8)
+        p_codes = tiles("p_codes", 4, [P, 2, 2 * N], U8)
+        ps_raw = one_tile("ps_raw", [P, A], U8)
+        ps_sorted = one_tile("ps_sorted", [P, A], U8)
+        p_scales = one_tile("p_scales", [P, 2, A], U8)
+        d_codes = tiles("d_codes", 4, [P, 2 * T], U8)
+        d_scales = one_tile("d_scales", [P, 4, T], U8)
+        lam_rows = one_tile("lam_rows", [P, N], BF16)
+        neg_lam = one_tile("neg_lam", [P, 16], F32)
+        time_g = one_tile("time_g", [P, T], BF16)
+        trace_g = one_tile("trace_g", [P, 8, 2], BF16)
+        upper = tiles("upper", UPPER_BUFS, [P, N], BF16)
+        h_rows = tiles("h_rows", UNIT_BUFS, [P, 4, N], BF16)
+        h_words = tiles("h_words", UNIT_BUFS, [P, 4 * N], BF16)
+        h_codes = tiles("h_codes", 8, [P, N], U32)
+        h_scales = tiles("h_scales", 8, [P, N], U8)
+        y = tiles("y", 16, [P, N], F32)
+        y_bf = tiles("y_bf", 16, [P, N], BF16)
+        y_words = tiles("y_words", 4, [P, 4 * N], BF16)
+        y_codes = one_tile("y_codes", [P, 2, M], U32)
+        y_scales = tiles("y_scales", 2, [P, 2, N], U8)
 
-        ident = sb.tile([P, P], F32, name="ident", align_bytes=64)
-        x_raw = tiles("x_raw", 8, [P, 2, 512], BF16)
-        x_grp = tiles("x_grp", 4, [P, 2048], BF16)
-        x_codes = tiles("x_codes", 4, [P, 512], U32)
-        x_scales = tiles("x_scales", 4, [P, 512], U8)
-        p_raw = tiles("p_raw", 4, [P, 2, 1024], U8)
-        p_words = tiles("p_words", 4, [P, 2, 1024], U8)
-        ps_raw = sb.tile([P, A], U8, name="ps_raw", align_bytes=64)
-        ps_ord = sb.tile([P, A], U8, name="ps_ord", align_bytes=64)
-        p_scales = sb.tile([P, 2, A], U8, name="p_scales", align_bytes=64)
-        d_words = tiles("d_words", 4, [P, 2048], U8)
-        d_scales = sb.tile([P, 4, T], U8, name="d_scales", align_bytes=64)
-        lam_rows = sb.tile([P, 512], BF16, name="lam_rows", align_bytes=64)
-        neg_lam = sb.tile([P, 16], F32, name="neg_lam", align_bytes=64)
-        tg = sb.tile([P, T], BF16, name="tg", align_bytes=64)
-        trg = sb.tile([P, 8, 2], BF16, name="trg", align_bytes=64)
-        upper = tiles("upper", 4, [P, 512], BF16)
-        h_rows = tiles("h_rows", 3, [P, 4, 512], BF16)
-        h_grp = tiles("h_grp", 3, [P, 2048], BF16)
-        h_codes = tiles("h_codes", 8, [P, 512], U32)
-        h_scales = tiles("h_scales", 8, [P, 512], U8)
-        y = tiles("y", 16, [P, 512], F32)
-        y_bf = tiles("y_bf", 15, [P, 512], BF16)
-        y_grp = tiles("y_grp", 4, [P, 2048], BF16)
-        y_codes = sb.tile([P, 2, M], U32, name="y_codes", align_bytes=64)
-        y_scales = tiles("y_scales", 2, [P, 2, 512], U8)
+        free_banks = list(range(PSUM_BANKS))
+        bank_of = {}
 
-        held = {}
+        def take_bank(user):
+            bank_of[user] = free_banks[0]
+            free_banks.remove(bank_of[user])
+            return banks[bank_of[user]]
 
-        def take(key):
-            held[key] = free_banks[0]
-            free_banks.remove(held[key])
-            return banks[held[key]]
-
-        def give(key):
-            free_banks.append(held[key])
-            return banks[held[key]]
+        def free_bank(user):
+            free_banks.append(bank_of[user])
+            return banks[bank_of[user]]
 
         def copy_on(engine, dst, src):
-            if engine == "V":
+            if engine is nc.vector:
                 nc.vector.tensor_copy(out=dst, in_=src)
-            elif engine == "S":
+            elif engine is nc.scalar:
                 nc.scalar.copy(out=dst, in_=src)
             else:
                 nc.gpsimd.tensor_scalar(out=dst, in0=src, scalar1=1.0, scalar2=0.0, op0=ALU.mult, op1=ALU.add)
 
+        def zero(engine, region):
+            engine.memset(region.bitcast(I32), 0)
+
+
         def load_x(b, g):
-            src = traces[256 * b : 256 * (b + 1), 512 * g : 512 * (g + 1)]
+            src = traces[2 * P * b : 2 * P * (b + 1), N * g : N * (g + 1)]
             nc.sync.dma_start(out=x_raw[2 * b + g][:], in_=src.rearrange("(e p) c -> p e c", p=P))
 
         def load_p(a):
-            src = pinv_words[:, :, 1024 * a : 1024 * (a + 1)].rearrange("g p c -> p g c")
+            src = pinv_words[:, :, 2 * N * a : 2 * N * (a + 1)].rearrange("g p c -> p g c")
             nc.sync.dma_start(out=p_raw[a][:].bitcast(I32), in_=src.bitcast(I32))
 
-        def load_scales(plane, scales):
-            for q in range(4):
-                src = scales[:, 4 * q : 4 * q + 4, :].rearrange("g r c -> r g c")
-                nc.sync.dma_start(out=plane[32 * q : 32 * q + 4, :, :].bitcast(I32), in_=src.bitcast(I32))
+        def load_d():
+            for quad in range(4):
+                src = dict_scales[:, 4 * quad : 4 * quad + 4, :].rearrange("a r c -> r a c")
+                nc.sync.dma_start(out=d_scales[32 * quad : 32 * quad + 4, :, :].bitcast(I32), in_=src.bitcast(I32))
+            for a in range(4):
+                nc.sync.dma_start(out=d_codes[a][:].bitcast(I32), in_=dict_words[a].bitcast(I32))
 
-        def load_d(a):
-            nc.sync.dma_start(out=d_words[a][:].bitcast(I32), in_=dict_words[a].bitcast(I32))
 
-        def thresholds():
-            bank = take("lam")
+        def sort_p_codes(a):
+            nc.vector.tensor_copy(
+                out=p_codes[a][:].rearrange("p g (j m e) -> p g j m e", j=4, e=2),
+                in_=p_raw[a][:].rearrange("p g (m j e) -> p g j m e", j=4, e=2),
+            )
+
+        def sort_p_scales():
+            nc.vector.tensor_copy(
+                out=ps_sorted[:].rearrange("p (a j m) -> p a j m", j=4, m=P),
+                in_=ps_raw[:].rearrange("p (a m j) -> p a j m", j=4, m=P),
+            )
+
+        def spread_p_scales():
+            for g in range(2):
+                for quad in range(4):
+                    row = 16 * g + 4 * quad
+                    nc.sync.dma_start(
+                        out=p_scales[32 * quad : 32 * quad + 4, g, :].bitcast(I32),
+                        in_=ps_sorted[row : row + 4, :].bitcast(I32),
+                    )
+
+
+        def make_neg_lam():
+            bank = take_bank("lam")
             words = lam_rows[:].bitcast(F32)
             for u in range(2):
-                nc.tensor.transpose(bank[:, P * u : P * (u + 1)], words[:, u:256:2], ident[:])
-            give("lam")
+                nc.tensor.transpose(bank[:, P * u : P * (u + 1)], words[:, u : 2 * P : 2], ident[:])
+            free_bank("lam")
             nc.scalar.activation(
                 out=neg_lam[:].rearrange("p (a u e) -> p a u e", u=2, e=2),
                 in_=bank[:, 0 : 2 * P].bitcast(BF16).rearrange("p (u r e) -> p r u e", u=2, e=2)[:, 0:4, :, :],
@@ -427,53 +149,37 @@ def tile_pinv_shrink_seismic_traces_h1_kernel(
             )
 
         def turn_x(b, g):
-            bank = take(("x", b, g))
+            bank = take_bank(("x", b, g))
             words = x_raw[2 * b + g][:].rearrange("p e c -> p (e c)").bitcast(F32)
             for e in range(2):
                 for u in range(2):
-                    k = 2 * e + u
-                    nc.tensor.transpose(bank[:, P * k : P * (k + 1)], words[:, 256 * e + u : 256 * (e + 1) : 2], ident[:])
+                    out = bank[:, P * (2 * e + u) : P * (2 * e + u + 1)]
+                    nc.tensor.transpose(out, words[:, 2 * P * e + u : 2 * P * (e + 1) : 2], ident[:])
 
-        def empty_x(b, g, engine):
-            bank = give(("x", b, g))
-            dst = x_grp[2 * (b // 2) + g][:].bitcast(F32)[:, 512 * (b % 2) : 512 * (b % 2 + 1)]
+        def empty_turned(user, engine, dst, count):
+            bank = free_bank(user)
             copy_on(
                 engine,
-                dst.rearrange("p (e m u) -> p e m u", e=2, u=2),
-                bank[:].rearrange("p (e u m) -> p e m u", e=2, u=2),
+                dst.bitcast(F32).rearrange("p (e m u) -> p e m u", e=count, u=2),
+                bank[:, 0 : 2 * P * count].rearrange("p (e u m) -> p e m u", e=count, u=2),
             )
+
+        def empty_x(b, g, engine):
+            dst = x_words[2 * (b // 2) + g][:, 2 * N * (b % 2) : 2 * N * (b % 2 + 1)]
+            empty_turned(("x", b, g), engine, dst, 2)
 
         def quant_x(h, g):
             k = 2 * h + g
-            nc.vector.quantize_mx(out=x_codes[k][:].bitcast(FP8X4), scales=x_scales[k][:], in_=x_grp[k][:])
+            nc.vector.quantize_mx(out=x_codes[k][:].bitcast(FP8X4), scales=x_scales[k][:], in_=x_words[k][:])
 
-        def order_p_words(a, g0, count):
-            nc.vector.tensor_copy(
-                out=p_words[a][:, g0 : g0 + count, :].rearrange("p g (j m e) -> p g j m e", j=4, e=2),
-                in_=p_raw[a][:, g0 : g0 + count, :].rearrange("p g (m j e) -> p g j m e", j=4, e=2),
-            )
-
-        def order_p_scales(a, count):
-            nc.vector.tensor_copy(
-                out=ps_ord[:].rearrange("p (a j m) -> p a j m", j=4, m=P),
-                in_=ps_raw[:].rearrange("p (a m j) -> p a j m", j=4, m=P),
-            )
-
-        def spread_p_scales():
-            for g in range(2):
-                for q in range(4):
-                    row = 16 * g + 4 * q
-                    nc.sync.dma_start(
-                        out=p_scales[32 * q : 32 * q + 4, g, :].bitcast(I32), in_=ps_ord[row : row + 4, :].bitcast(I32)
-                    )
 
         def codes_pass(s, g):
             h, a, j = s // 16, (s // 4) % 4, s % 4
-            bank = take(("c", s)) if g == 0 else banks[held[("c", s)]]
-            col = 512 * a + P * j
+            bank = take_bank(("c", s)) if g == 0 else banks[bank_of[("c", s)]]
+            col = N * a + P * j
             nc.tensor.matmul_mx(
                 out=bank[:],
-                lhsT=p_words[a][:, g, 256 * j : 256 * (j + 1)].bitcast(FP4X4),
+                lhsT=p_codes[a][:, g, 2 * P * j : 2 * P * (j + 1)].bitcast(FP4X4),
                 lhsT_scale=p_scales[:, g, col : col + P],
                 rhs=x_codes[2 * h + g][:].bitcast(FP8X4),
                 rhs_scale=x_scales[2 * h + g][:],
@@ -481,176 +187,276 @@ def tile_pinv_shrink_seismic_traces_h1_kernel(
                 stop=(g == 1),
             )
 
+
         def relu(s):
             col = s % 16
-            bank = banks[held[("c", s)]]
             nc.scalar.activation(
-                out=upper[s % 4][:], in_=bank[:], func=ACT.Relu, bias=neg_lam[:, col : col + 1], scale=1.0
+                out=upper[s % UPPER_BUFS][:],
+                in_=banks[bank_of[("c", s)]][:],
+                func=ACT.Relu,
+                bias=neg_lam[:, col : col + 1],
+                scale=1.0,
             )
 
         def shrink(s):
-            n, j = s // 4, s % 4
             col = s % 16
-            bank = give(("c", s))
             nc.vector.scalar_tensor_tensor(
-                out=h_rows[n % 3][:, j, :],
-                in0=bank[:],
+                out=h_rows[(s // 4) % UNIT_BUFS][:, s % 4, :],
+                in0=free_bank(("c", s))[:],
                 scalar=neg_lam[:, col : col + 1],
-                in1=upper[s % 4][:],
+                in1=upper[s % UPPER_BUFS][:],
                 op0=ALU.subtract,
                 op1=ALU.min,
             )
 
-        def interleave(n, q, count, engine):
-            dst = h_grp[n % 3][:, 512 * q : 512 * (q + count)]
-            src = h_rows[n % 3][:, :, P * q : P * (q + count)]
-            if engine == "G":
-                copy_on(engine, dst.rearrange("p (c t) -> p c t", t=4), src.rearrange("p t c -> p c t"))
-            else:
+        def interleave_on_scalar(n):
+            count = QUARTERS_ON_SCALAR[n]
+            nc.scalar.copy(
+                out=h_words[n % UNIT_BUFS][:, 0 : N * count].rearrange("p (c m j) -> p c j m", m=4, j=4),
+                in_=h_rows[n % UNIT_BUFS][:, :, 0 : P * count].rearrange("p j (c m) -> p c j m", m=4),
+            )
+
+        def interleave_on_gpsimd(n):
+            for quarter in range(QUARTERS_ON_SCALAR[n], 4):
                 copy_on(
-                    engine,
-                    dst.rearrange("p (c i t) -> p c t i", i=4, t=4),
-                    src.rearrange("p t (c i) -> p c t i", i=4),
+                    nc.gpsimd,
+                    h_words[n % UNIT_BUFS][:, N * quarter : N * (quarter + 1)].rearrange("p (m j) -> p m j", j=4),
+                    h_rows[n % UNIT_BUFS][:, :, P * quarter : P * (quarter + 1)].rearrange("p j m -> p m j"),
                 )
 
         def quant_h(n):
-            nc.vector.quantize_mx(out=h_codes[n][:].bitcast(FP8X4), scales=h_scales[n][:], in_=h_grp[n % 3][:])
-
-        def rebuild_pass(i, g, a):
-            bank = take(("r", i, g)) if a == 0 else banks[held[("r", i, g)]]
-            n = 4 * (i // 4) + a
-            cols = slice(P * (i % 4), P * (i % 4 + 1))
-            nc.tensor.matmul_mx(
-                out=bank[:],
-                lhsT=h_codes[n][:, cols].bitcast(FP8X4),
-                lhsT_scale=h_scales[n][:, cols],
-                rhs=d_words[a][:, 1024 * g : 1024 * (g + 1)].bitcast(FP4X4),
-                rhs_scale=d_scales[:, a, 512 * g : 512 * (g + 1)],
-                start=(a == 0),
-                stop=(a == 3),
+            nc.vector.quantize_mx(
+                out=h_codes[n][:].bitcast(FP8X4), scales=h_scales[n][:], in_=h_words[n % UNIT_BUFS][:]
             )
 
-        def apply_gains(i, g, dst):
+
+        def rebuild(block, first_a, end_a):
+            i, g = block
+            cols = slice(P * (i % 4), P * (i % 4 + 1))
+            for a in range(first_a, end_a):
+                bank = take_bank(("r", block)) if a == 0 else banks[bank_of[("r", block)]]
+                n = 4 * (i // 4) + a
+                nc.tensor.matmul_mx(
+                    out=bank[:],
+                    lhsT=h_codes[n][:, cols].bitcast(FP8X4),
+                    lhsT_scale=h_scales[n][:, cols],
+                    rhs=d_codes[a][:, 2 * N * g : 2 * N * (g + 1)].bitcast(FP4X4),
+                    rhs_scale=d_scales[:, a, N * g : N * (g + 1)],
+                    start=(a == 0),
+                    stop=(a == 3),
+                )
+
+        def apply_gains(block, dst):
+            i, g = block
             nc.vector.scalar_tensor_tensor(
                 out=dst,
-                in0=banks[held[("r", i, g)]][:],
-                scalar=trg[:, i, 0:1],
-                in1=tg[:, 512 * g : 512 * (g + 1)],
+                in0=banks[bank_of[("r", block)]][:],
+                scalar=trace_g[:, i, 0:1],
+                in1=time_g[:, N * g : N * (g + 1)],
                 op0=ALU.mult,
                 op1=ALU.mult,
             )
 
-        def gain(i, g):
-            dst = y[2 * i + g][:]
-            apply_gains(i, g, dst)
-            give(("r", i, g))
-            nc.sync.dma_start(out=out_0[P * i : P * (i + 1), 512 * g : 512 * (g + 1)], in_=dst)
+        def gain(block):
+            i, g = block
+            apply_gains(block, y[2 * i + g][:])
+            free_bank(("r", block))
+            nc.sync.dma_start(out=out_0[P * i : P * (i + 1), N * g : N * (g + 1)], in_=y[2 * i + g][:])
 
-        def gain_bf(i, g):
-            apply_gains(i, g, last_bf[:])
 
-        last_bf = sb.tile([P, 512], BF16, name="last_bf", align_bytes=64)
-
-        def cast_y(i, g, count, engine):
-            dst = y_bf[2 * i + g][:].rearrange("p (u w x) -> p u w x", u=2, x=2)
-            src = y[2 * i + g][:].rearrange("p (w u x) -> p u w x", u=2, x=2)
-            copy_on(engine, dst, src)
-
-        def turn_y(i, count, g):
-            bank = take(("y", i, g))
-            for e in range(count):
-                for u in range(2):
-                    k = 2 * e + u
-                    if (i + e, g) == (7, 1):
-                        src = last_bf[:].bitcast(F32)[:, u:256:2]
-                    else:
-                        src = y_bf[2 * (i + e) + g][:].bitcast(F32)[:, P * u : P * (u + 1)]
-                    nc.tensor.transpose(bank[:, P * k : P * (k + 1)], src, ident[:])
-
-        def y_stage(i, count, g):
-            return y_grp[2 * (i // 4) + g][:, 512 * (i % 4) : 512 * (i % 4 + count)]
-
-        def empty_y(i, count, g, engine):
-            bank = give(("y", i, g))
+        def round_y(block, engine):
+            k = 2 * block[0] + block[1]
             copy_on(
                 engine,
-                y_stage(i, count, g).bitcast(F32).rearrange("p (e m u) -> p e m u", e=count, u=2),
-                bank[:, 0 : 256 * count].rearrange("p (e u m) -> p e m u", e=count, u=2),
+                y_bf[k][:].rearrange("p (u w e) -> p u w e", u=2, e=2),
+                y[k][:].rearrange("p (w u e) -> p u w e", u=2, e=2),
             )
+
+        def round_last_from_psum():
+            apply_gains(LAST, y_bf[2 * LAST[0] + LAST[1]][:])
+
+        def turn_y(i, count, g):
+            bank = take_bank(("y", i, g))
+            for e in range(count):
+                words = y_bf[2 * (i + e) + g][:].bitcast(F32)
+                for u in range(2):
+                    src = words[:, u : 2 * P : 2] if (i + e, g) == LAST else words[:, P * u : P * (u + 1)]
+                    nc.tensor.transpose(bank[:, P * (2 * e + u) : P * (2 * e + u + 1)], src, ident[:])
+
+        def y_window(i, count, g):
+            return y_words[2 * (i // 4) + g][:, N * (i % 4) : N * (i % 4 + count)]
+
+        def empty_y(i, count, g):
+            empty_turned(("y", i, g), nc.scalar, y_window(i, count, g), count)
 
         def quant_y(i, count, g):
             cols = slice(P * i, P * (i + count))
             nc.vector.quantize_mx(
-                out=y_codes[:, g, cols].bitcast(FP8X4), scales=y_scales[i // 4][:, g, P * (i % 4) : P * (i % 4 + count)], in_=y_stage(i, count, g)
+                out=y_codes[:, g, cols].bitcast(FP8X4),
+                scales=y_scales[i // 4][:, g, P * (i % 4) : P * (i % 4 + count)],
+                in_=y_window(i, count, g),
             )
+
+        def store_y_codes(i, count, g):
+            cols = slice(P * i, P * (i + count))
             dst = out_1[g, :, cols, :].rearrange("p m t -> p (m t)")
             nc.sync.dma_start(out=dst.bitcast(I32), in_=y_codes[:, g, cols].bitcast(I32))
 
-        def store_scales(m0, m1, queues):
-            for q in range(4):
-                dst = out_2[:, 4 * q : 4 * q + 4, m0:m1].rearrange("g r c -> r g c")
-                queues[q % 2].dma_start(
-                    out=dst.bitcast(I32), in_=y_scales[m0 // 512][32 * q : 32 * q + 4, :, :].bitcast(I32)
-                )
+        def store_y_scales(h, queues):
+            for quad in range(4):
+                dst = out_2[:, 4 * quad : 4 * quad + 4, N * h : N * (h + 1)].rearrange("g r c -> r g c")
+                src = y_scales[h][32 * quad : 32 * quad + 4, :, :]
+                queues[quad % 2].dma_start(out=dst.bitcast(I32), in_=src.bitcast(I32))
 
-        def early_scales(m1):
-            store_scales(0, m1, (nc.sync, nc.sync))
-
-        def zero_d():
-            zero(nc.vector, d_scales[:].rearrange("p g c -> p (g c)"))
-
-        def zero(engine, tile):
-            engine.memset(tile.bitcast(I32), 0)
-
+        zero(nc.gpsimd, lam_rows[:])
+        zero(nc.gpsimd, ps_raw[:])
         make_identity(nc, ident[:])
-        zero(nc.vector, lam_rows[:])
-        zero(nc.vector, ps_raw[:])
         zero(nc.vector, p_scales[:].rearrange("p g c -> p (g c)"))
-        zero_d()
+        zero(nc.vector, d_scales[:].rearrange("p a c -> p (a c)"))
         nc.scalar.dma_start(out=lam_rows[0:4, :], in_=lam.rearrange("(a c) -> a c", a=4))
         load_x(0, 0)
         nc.sync.dma_start(out=ps_raw[0:32, :].bitcast(I32), in_=pinv_scales.rearrange("g q c -> (g q) c").bitcast(I32))
-        order_p_scales(0, 1)
+        sort_p_scales()
         load_p(0)
         load_x(1, 0)
         load_p(1)
         load_x(0, 1)
         load_x(1, 1)
         spread_p_scales()
-        load_p(2)
-        for g in range(2):
-            for b in range(2, 4):
-                load_x(b, g)
-            if g == 0:
-                load_p(3)
-        load_scales(d_scales, dict_scales)
-        for a in range(4):
-            load_d(a)
-        nc.sync.dma_start(out=tg[:], in_=time_gain.partition_broadcast(P))
+        for g in (1, 0):
+            load_p(3 - g)
+            load_x(2, g)
+            load_x(3, g)
+        load_d()
+        nc.sync.dma_start(out=time_g[:], in_=time_gain.partition_broadcast(P))
         with nc.allow_non_contiguous_dma(reason="one gain for each partition"):
-            nc.sync.dma_start(out=trg[:, :, 0:1], in_=trace_gain.rearrange("(i p o) -> p i o", p=P, o=1))
+            nc.sync.dma_start(out=trace_g[:, :, 0:1], in_=trace_gain.rearrange("(i p o) -> p i o", p=P, o=1))
 
-        table = {
-            "turn_x": turn_x,
-            "empty_x": empty_x,
-            "quant_x": quant_x,
-            "order_p_words": order_p_words,
-            "order_p_scales": order_p_scales,
-            "thresholds": thresholds,
-            "codes_pass": codes_pass,
-            "relu": relu,
-            "shrink": shrink,
-            "interleave": interleave,
-            "quant_h": quant_h,
-            "rebuild_pass": rebuild_pass,
-            "gain": gain,
-            "gain_bf": gain_bf,
-            "cast_y": cast_y,
-            "turn_y": turn_y,
-            "empty_y": empty_y,
-            "quant_y": quant_y,
-            "early_scales": early_scales,
-        }
-        for step in ORDER:
-            table[step[0]](*step[1:])
-        store_scales(512, M, (nc.scalar, nc.sync))
+        for g in range(2):
+            sort_p_codes(g)
+            for b in range(2):
+                turn_x(b, g)
+                if (b, g) == (0, 0):
+                    make_neg_lam()
+                empty_x(b, g, nc.scalar)
+            quant_x(0, g)
+        sort_p_codes(2)
+        sort_p_codes(3)
+        for s in range(4):
+            codes_pass(s, 0)
+
+        after = {s: [] for s in range(SLOTS)}
+
+        def place(s, step, *args):
+            after[s].append((step, args))
+
+        for g, s in ((0, 4), (1, 2)):
+            for b in (2, 3):
+                place(s, turn_x, b, g)
+            for b in (2, 3):
+                place(s + 2, empty_x, b, g, nc.vector if (b, g) == (2, 0) else nc.scalar)
+        place(10, quant_x, 1, 0)
+        place(7, quant_x, 1, 1)
+        for n in range(7):
+            place(QUANT_H_AFTER[n], quant_h, n)
+        for n in range(7):
+            if QUARTERS_ON_SCALAR[n] > 0:
+                place(4 * n + SCALAR_QUARTERS_AFTER[n], interleave_on_scalar, n)
+            place(4 * n + 3, interleave_on_gpsimd, n)
+
+        blocks = [(i, g) for b in range(4) for g in range(2) for i in (2 * b, 2 * b + 1)]
+        for k, s in enumerate((14, 16, 18)):
+            place(s, rebuild, blocks[k], 0, 2)
+        for k, s in enumerate((17, 17, 18)):
+            place(s, rebuild, blocks[k], 2, 3)
+        for k, s in enumerate((20, 20, 21)):
+            place(s, rebuild, blocks[k], 3, 4)
+        for k, s in enumerate((22, 23, 24)):
+            place(s, gain, blocks[k])
+        for k, s in enumerate((22, 26, 26, 28, 29)):
+            place(s, rebuild, blocks[3 + k], 0, 4)
+        place(28, gain, blocks[3])
+        place(24, round_y, blocks[0], nc.scalar)
+        place(23, round_y, blocks[1], nc.gpsimd)
+        place(28, round_y, blocks[2], nc.scalar)
+
+        for s in range(-CODES_AHEAD, SLOTS):
+            ahead = s + CODES_AHEAD
+            if ahead < SLOTS:
+                if ahead >= 4:
+                    codes_pass(ahead, 0)
+                codes_pass(ahead, 1)
+            if 0 <= s + RELU_AHEAD < SLOTS:
+                relu(s + RELU_AHEAD)
+            if s >= 0:
+                shrink(s)
+                for step, args in after[s]:
+                    step(*args)
+
+        interleave_on_scalar(7)
+        interleave_on_gpsimd(7)
+        round_y(blocks[3], nc.scalar)
+        gain(blocks[4])
+        gain(blocks[5])
+        for k in range(8, 12):
+            rebuild(blocks[k], 0, 2)
+        quant_h(7)
+        gain(blocks[6])
+        gain(blocks[7])
+        round_y(blocks[4], nc.scalar)
+        round_y(blocks[5], nc.scalar)
+        for k in (8, 9):
+            rebuild(blocks[k], 2, 3)
+        for g in range(2):
+            turn_y(0, 2, g)
+        for k in (10, 11):
+            rebuild(blocks[k], 2, 3)
+        for k in range(8, 12):
+            rebuild(blocks[k], 3, 4)
+        for g in range(2):
+            empty_y(0, 2, g)
+        round_y(blocks[6], nc.gpsimd)
+        round_y(blocks[7], nc.gpsimd)
+        for k in range(8, 12):
+            gain(blocks[k])
+        round_y(blocks[8], nc.scalar)
+        round_y(blocks[9], nc.gpsimd)
+        rebuild(blocks[12], 0, 4)
+        for g in range(2):
+            turn_y(2, 2, g)
+        gain(blocks[12])
+        round_y(blocks[10], nc.scalar)
+        round_y(blocks[11], nc.gpsimd)
+        rebuild(blocks[13], 0, 4)
+        rebuild(blocks[14], 0, 4)
+        for g in range(2):
+            empty_y(2, 2, g)
+        gain(blocks[13])
+        quant_y(0, 4, 0)
+        store_y_codes(0, 4, 0)
+        round_y(blocks[12], nc.scalar)
+        gain(blocks[14])
+        round_y(blocks[13], nc.scalar)
+        rebuild(LAST, 0, 4)
+        round_y(blocks[14], nc.gpsimd)
+        quant_y(0, 4, 1)
+        store_y_codes(0, 4, 1)
+        store_y_scales(0, (nc.sync, nc.sync))
+        pieces = [(4, 2, 0), (4, 2, 1), (6, 2, 0), (6, 1, 1), (7, 1, 1)]
+        for piece in pieces[:2]:
+            turn_y(*piece)
+        round_last_from_psum()
+        gain(LAST)
+        for piece in pieces[2:]:
+            turn_y(*piece)
+        for piece in pieces:
+            empty_y(*piece)
+        for piece in pieces[:2]:
+            quant_y(*piece)
+        store_y_codes(4, 2, 1)
+        quant_y(*pieces[2])
+        store_y_codes(4, 4, 0)
+        for piece in pieces[3:]:
+            quant_y(*piece)
+        store_y_codes(6, 2, 1)
+        store_y_scales(1, (nc.scalar, nc.sync))

@@ -27,6 +27,8 @@ RELU_AHEAD = 3
 QUARTERS_ON_SCALAR = (0, 2, 2, 1, 0, 3, 1, 2)
 SCALAR_QUARTERS_AFTER = (3, 5, 4, 4, 3, 3, 3)
 QUANT_H_AFTER = (10, 11, 15, 19, 25, 27, 31)
+WARM_FIRST = 18
+WARM_AGAIN = 8
 LAST = (7, 1)
 
 
@@ -71,6 +73,8 @@ def tile_pinv_shrink_seismic_traces_h1_kernel(
         y_bf = tiles("y_bf", 16, [P, N], BF16)
         y_words = tiles("y_words", 4, [P, 4 * N], BF16)
         y_codes = one_tile("y_codes", [P, 2, M], U32)
+        warm_codes = one_tile("warm_codes", [P, P], U32)
+        warm_scales = one_tile("warm_scales", [P, P], U8)
         y_scales = tiles("y_scales", 2, [P, 2, N], U8)
 
         free_banks = list(range(PSUM_BANKS))
@@ -308,9 +312,23 @@ def tile_pinv_shrink_seismic_traces_h1_kernel(
                 src = y_scales[h][32 * quad : 32 * quad + 4, :, :]
                 queues[quad % 2].dma_start(out=dst.bitcast(I32), in_=src.bitcast(I32))
 
+        def warm_up(count):
+            for k in range(count):
+                nc.tensor.matmul_mx(
+                    out=banks[PSUM_BANKS - 1][:, P * (k % 4) : P * (k % 4 + 1)],
+                    lhsT=warm_codes[:, 0 : P // 2].bitcast(U8).bitcast(FP4X4),
+                    lhsT_scale=warm_scales[:],
+                    rhs=warm_codes[:].bitcast(FP8X4),
+                    rhs_scale=warm_scales[:],
+                    start=True,
+                    stop=True,
+                )
+
         zero(nc.gpsimd, lam_rows[:])
         zero(nc.gpsimd, ps_raw[:])
         make_identity(nc, ident[:])
+        nc.vector.quantize_mx(out=warm_codes[:].bitcast(FP8X4), scales=warm_scales[:], in_=lam_rows[:])
+        warm_up(WARM_FIRST)
         zero(nc.vector, p_scales[:].rearrange("p g c -> p (g c)"))
         zero(nc.vector, d_scales[:].rearrange("p a c -> p (a c)"))
         nc.scalar.dma_start(out=lam_rows[0:4, :], in_=lam.rearrange("(a c) -> a c", a=4))
@@ -339,6 +357,7 @@ def tile_pinv_shrink_seismic_traces_h1_kernel(
                 if (b, g) == (0, 0):
                     make_neg_lam()
                 empty_x(b, g, nc.scalar)
+            warm_up(WARM_AGAIN)
             quant_x(0, g)
         sort_p_codes(2)
         sort_p_codes(3)

from contextlib import ExitStack

import concourse.mybir as mybir
from concourse.masks import make_identity

F32 = mybir.dt.float32
BF16 = mybir.dt.bfloat16
U32 = mybir.dt.uint32
I32 = mybir.dt.int32
U8 = mybir.dt.uint8
FP8X4 = mybir.dt.float8_e4m3fn_x4
FP4X4 = mybir.dt.float4_e2m1fn_x4
ALU = mybir.AluOpType
ACT = mybir.ActivationFunctionType

M, T, A = 1024, 1024, 2048
FLOPS = 4 * M * T * A

P = 128
N = 512
SLOTS = 32
PSUM_BANKS = 8
UPPER_BUFS = 4
UNIT_BUFS = 3
CODES_AHEAD = 4
RELU_AHEAD = 3
QUARTERS_ON_SCALAR = (0, 2, 2, 1, 0, 3, 1, 2)
SCALAR_QUARTERS_AFTER = (3, 5, 4, 4, 3, 3, 3)
QUANT_H_AFTER = (10, 11, 15, 19, 25, 27, 31)
WARM_FIRST = 18
WARM_AGAIN = 8
LAST = (7, 1)


def tile_pinv_shrink_seismic_traces_h1_kernel(
    tc, traces, pinv_words, pinv_scales, lam, dict_words, dict_scales, time_gain, trace_gain, out_0, out_1, out_2
):
    nc = tc.nc
    with ExitStack() as ctx:
        sb = ctx.enter_context(tc.tile_pool(name="sb", bufs=1))
        pp = ctx.enter_context(tc.psum_pool(name="pp", bufs=1))
        ctx.enter_context(tc.manual_schedule())

        def one_tile(name, shape, dtype):
            return sb.tile(shape, dtype, name=name, align_bytes=64)

        def tiles(name, count, shape, dtype):
            return [one_tile("%s%d" % (name, k), shape, dtype) for k in range(count)]

        banks = [pp.tile([P, N], F32, name="bank%d" % k) for k in range(PSUM_BANKS)]
        ident = one_tile("ident", [P, P], F32)
        x_raw = tiles("x_raw", 8, [P, 2, N], BF16)
        x_words = tiles("x_words", 4, [P, 4 * N], BF16)
        x_codes = tiles("x_codes", 4, [P, N], U32)
        x_scales = tiles("x_scales", 4, [P, N], U8)
        p_raw = tiles("p_raw", 4, [P, 2, 2 * N], U8)
        p_codes = tiles("p_codes", 4, [P, 2, 2 * N], U8)
        ps_raw = one_tile("ps_raw", [P, A], U8)
        ps_sorted = one_tile("ps_sorted", [P, A], U8)
        p_scales = one_tile("p_scales", [P, 2, A], U8)
        d_codes = tiles("d_codes", 4, [P, 2 * T], U8)
        d_scales = one_tile("d_scales", [P, 4, T], U8)
        lam_rows = one_tile("lam_rows", [P, N], BF16)
        neg_lam = one_tile("neg_lam", [P, 16], F32)
        time_g = one_tile("time_g", [P, T], BF16)
        trace_g = one_tile("trace_g", [P, 8, 2], BF16)
        upper = tiles("upper", UPPER_BUFS, [P, N], BF16)
        h_rows = tiles("h_rows", UNIT_BUFS, [P, 4, N], BF16)
        h_words = tiles("h_words", UNIT_BUFS, [P, 4 * N], BF16)
        h_codes = tiles("h_codes", 8, [P, N], U32)
        h_scales = tiles("h_scales", 8, [P, N], U8)
        y = tiles("y", 16, [P, N], F32)
        y_bf = tiles("y_bf", 16, [P, N], BF16)
        y_words = tiles("y_words", 4, [P, 4 * N], BF16)
        y_codes = one_tile("y_codes", [P, 2, M], U32)
        warm_codes = one_tile("warm_codes", [P, P], U32)
        warm_scales = one_tile("warm_scales", [P, P], U8)
        y_scales = tiles("y_scales", 2, [P, 2, N], U8)

        free_banks = list(range(PSUM_BANKS))
        bank_of = {}

        def take_bank(user):
            bank_of[user] = free_banks[0]
            free_banks.remove(bank_of[user])
            return banks[bank_of[user]]

        def free_bank(user):
            free_banks.append(bank_of[user])
            return banks[bank_of[user]]

        def copy_on(engine, dst, src):
            if engine is nc.vector:
                nc.vector.tensor_copy(out=dst, in_=src)
            elif engine is nc.scalar:
                nc.scalar.copy(out=dst, in_=src)
            else:
                nc.gpsimd.tensor_scalar(out=dst, in0=src, scalar1=1.0, scalar2=0.0, op0=ALU.mult, op1=ALU.add)

        def zero(engine, region):
            engine.memset(region.bitcast(I32), 0)


        def load_x(b, g):
            src = traces[2 * P * b : 2 * P * (b + 1), N * g : N * (g + 1)]
            nc.sync.dma_start(out=x_raw[2 * b + g][:], in_=src.rearrange("(e p) c -> p e c", p=P))

        def load_p(a):
            src = pinv_words[:, :, 2 * N * a : 2 * N * (a + 1)].rearrange("g p c -> p g c")
            nc.sync.dma_start(out=p_raw[a][:].bitcast(I32), in_=src.bitcast(I32))

        def load_d():
            for quad in range(4):
                src = dict_scales[:, 4 * quad : 4 * quad + 4, :].rearrange("a r c -> r a c")
                nc.sync.dma_start(out=d_scales[32 * quad : 32 * quad + 4, :, :].bitcast(I32), in_=src.bitcast(I32))
            for a in range(4):
                nc.sync.dma_start(out=d_codes[a][:].bitcast(I32), in_=dict_words[a].bitcast(I32))


        def sort_p_codes(a):
            nc.vector.tensor_copy(
                out=p_codes[a][:].rearrange("p g (j m e) -> p g j m e", j=4, e=2),
                in_=p_raw[a][:].rearrange("p g (m j e) -> p g j m e", j=4, e=2),
            )

        def sort_p_scales():
            nc.vector.tensor_copy(
                out=ps_sorted[:].rearrange("p (a j m) -> p a j m", j=4, m=P),
                in_=ps_raw[:].rearrange("p (a m j) -> p a j m", j=4, m=P),
            )

        def spread_p_scales():
            for g in range(2):
                for quad in range(4):
                    row = 16 * g + 4 * quad
                    nc.sync.dma_start(
                        out=p_scales[32 * quad : 32 * quad + 4, g, :].bitcast(I32),
                        in_=ps_sorted[row : row + 4, :].bitcast(I32),
                    )


        def make_neg_lam():
            bank = take_bank("lam")
            words = lam_rows[:].bitcast(F32)
            for u in range(2):
                nc.tensor.transpose(bank[:, P * u : P * (u + 1)], words[:, u : 2 * P : 2], ident[:])
            free_bank("lam")
            nc.scalar.activation(
                out=neg_lam[:].rearrange("p (a u e) -> p a u e", u=2, e=2),
                in_=bank[:, 0 : 2 * P].bitcast(BF16).rearrange("p (u r e) -> p r u e", u=2, e=2)[:, 0:4, :, :],
                func=ACT.Copy,
                scale=-1.0,
            )

        def turn_x(b, g):
            bank = take_bank(("x", b, g))
            words = x_raw[2 * b + g][:].rearrange("p e c -> p (e c)").bitcast(F32)
            for e in range(2):
                for u in range(2):
                    out = bank[:, P * (2 * e + u) : P * (2 * e + u + 1)]
                    nc.tensor.transpose(out, words[:, 2 * P * e + u : 2 * P * (e + 1) : 2], ident[:])

        def empty_turned(user, engine, dst, count):
            bank = free_bank(user)
            copy_on(
                engine,
                dst.bitcast(F32).rearrange("p (e m u) -> p e m u", e=count, u=2),
                bank[:, 0 : 2 * P * count].rearrange("p (e u m) -> p e m u", e=count, u=2),
            )

        def empty_x(b, g, engine):
            dst = x_words[2 * (b // 2) + g][:, 2 * N * (b % 2) : 2 * N * (b % 2 + 1)]
            empty_turned(("x", b, g), engine, dst, 2)

        def quant_x(h, g):
            k = 2 * h + g
            nc.vector.quantize_mx(out=x_codes[k][:].bitcast(FP8X4), scales=x_scales[k][:], in_=x_words[k][:])


        def codes_pass(s, g):
            h, a, j = s // 16, (s // 4) % 4, s % 4
            bank = take_bank(("c", s)) if g == 0 else banks[bank_of[("c", s)]]
            col = N * a + P * j
            nc.tensor.matmul_mx(
                out=bank[:],
                lhsT=p_codes[a][:, g, 2 * P * j : 2 * P * (j + 1)].bitcast(FP4X4),
                lhsT_scale=p_scales[:, g, col : col + P],
                rhs=x_codes[2 * h + g][:].bitcast(FP8X4),
                rhs_scale=x_scales[2 * h + g][:],
                start=(g == 0),
                stop=(g == 1),
            )


        def relu(s):
            col = s % 16
            nc.scalar.activation(
                out=upper[s % UPPER_BUFS][:],
                in_=banks[bank_of[("c", s)]][:],
                func=ACT.Relu,
                bias=neg_lam[:, col : col + 1],
                scale=1.0,
            )

        def shrink(s):
            col = s % 16
            nc.vector.scalar_tensor_tensor(
                out=h_rows[(s // 4) % UNIT_BUFS][:, s % 4, :],
                in0=free_bank(("c", s))[:],
                scalar=neg_lam[:, col : col + 1],
                in1=upper[s % UPPER_BUFS][:],
                op0=ALU.subtract,
                op1=ALU.min,
            )

        def interleave_on_scalar(n):
            count = QUARTERS_ON_SCALAR[n]
            nc.scalar.copy(
                out=h_words[n % UNIT_BUFS][:, 0 : N * count].rearrange("p (c m j) -> p c j m", m=4, j=4),
                in_=h_rows[n % UNIT_BUFS][:, :, 0 : P * count].rearrange("p j (c m) -> p c j m", m=4),
            )

        def interleave_on_gpsimd(n):
            for quarter in range(QUARTERS_ON_SCALAR[n], 4):
                copy_on(
                    nc.gpsimd,
                    h_words[n % UNIT_BUFS][:, N * quarter : N * (quarter + 1)].rearrange("p (m j) -> p m j", j=4),
                    h_rows[n % UNIT_BUFS][:, :, P * quarter : P * (quarter + 1)].rearrange("p j m -> p m j"),
                )

        def quant_h(n):
            nc.vector.quantize_mx(
                out=h_codes[n][:].bitcast(FP8X4), scales=h_scales[n][:], in_=h_words[n % UNIT_BUFS][:]
            )


        def rebuild(block, first_a, end_a):
            i, g = block
            cols = slice(P * (i % 4), P * (i % 4 + 1))
            for a in range(first_a, end_a):
                bank = take_bank(("r", block)) if a == 0 else banks[bank_of[("r", block)]]
                n = 4 * (i // 4) + a
                nc.tensor.matmul_mx(
                    out=bank[:],
                    lhsT=h_codes[n][:, cols].bitcast(FP8X4),
                    lhsT_scale=h_scales[n][:, cols],
                    rhs=d_codes[a][:, 2 * N * g : 2 * N * (g + 1)].bitcast(FP4X4),
                    rhs_scale=d_scales[:, a, N * g : N * (g + 1)],
                    start=(a == 0),
                    stop=(a == 3),
                )

        def apply_gains(block, dst):
            i, g = block
            nc.vector.scalar_tensor_tensor(
                out=dst,
                in0=banks[bank_of[("r", block)]][:],
                scalar=trace_g[:, i, 0:1],
                in1=time_g[:, N * g : N * (g + 1)],
                op0=ALU.mult,
                op1=ALU.mult,
            )

        def gain(block):
            i, g = block
            apply_gains(block, y[2 * i + g][:])
            free_bank(("r", block))
            nc.sync.dma_start(out=out_0[P * i : P * (i + 1), N * g : N * (g + 1)], in_=y[2 * i + g][:])


        def round_y(block, engine):
            k = 2 * block[0] + block[1]
            copy_on(
                engine,
                y_bf[k][:].rearrange("p (u w e) -> p u w e", u=2, e=2),
                y[k][:].rearrange("p (w u e) -> p u w e", u=2, e=2),
            )

        def round_last_from_psum():
            apply_gains(LAST, y_bf[2 * LAST[0] + LAST[1]][:])

        def turn_y(i, count, g):
            bank = take_bank(("y", i, g))
            for e in range(count):
                words = y_bf[2 * (i + e) + g][:].bitcast(F32)
                for u in range(2):
                    src = words[:, u : 2 * P : 2] if (i + e, g) == LAST else words[:, P * u : P * (u + 1)]
                    nc.tensor.transpose(bank[:, P * (2 * e + u) : P * (2 * e + u + 1)], src, ident[:])

        def y_window(i, count, g):
            return y_words[2 * (i // 4) + g][:, N * (i % 4) : N * (i % 4 + count)]

        def empty_y(i, count, g):
            empty_turned(("y", i, g), nc.scalar, y_window(i, count, g), count)

        def quant_y(i, count, g):
            cols = slice(P * i, P * (i + count))
            nc.vector.quantize_mx(
                out=y_codes[:, g, cols].bitcast(FP8X4),
                scales=y_scales[i // 4][:, g, P * (i % 4) : P * (i % 4 + count)],
                in_=y_window(i, count, g),
            )

        def store_y_codes(i, count, g):
            cols = slice(P * i, P * (i + count))
            dst = out_1[g, :, cols, :].rearrange("p m t -> p (m t)")
            nc.sync.dma_start(out=dst.bitcast(I32), in_=y_codes[:, g, cols].bitcast(I32))

        def store_y_scales(h, queues):
            for quad in range(4):
                dst = out_2[:, 4 * quad : 4 * quad + 4, N * h : N * (h + 1)].rearrange("g r c -> r g c")
                src = y_scales[h][32 * quad : 32 * quad + 4, :, :]
                queues[quad % 2].dma_start(out=dst.bitcast(I32), in_=src.bitcast(I32))

        def warm_up(count):
            for k in range(count):
                nc.tensor.matmul_mx(
                    out=banks[PSUM_BANKS - 1][:, P * (k % 4) : P * (k % 4 + 1)],
                    lhsT=warm_codes[:, 0 : P // 2].bitcast(U8).bitcast(FP4X4),
                    lhsT_scale=warm_scales[:],
                    rhs=warm_codes[:].bitcast(FP8X4),
                    rhs_scale=warm_scales[:],
                    start=True,
                    stop=True,
                )

        zero(nc.gpsimd, lam_rows[:])
        zero(nc.gpsimd, ps_raw[:])
        make_identity(nc, ident[:])
        nc.vector.quantize_mx(out=warm_codes[:].bitcast(FP8X4), scales=warm_scales[:], in_=lam_rows[:])
        warm_up(WARM_FIRST)
        zero(nc.vector, p_scales[:].rearrange("p g c -> p (g c)"))
        zero(nc.vector, d_scales[:].rearrange("p a c -> p (a c)"))
        nc.scalar.dma_start(out=lam_rows[0:4, :], in_=lam.rearrange("(a c) -> a c", a=4))
        load_x(0, 0)
        nc.sync.dma_start(out=ps_raw[0:32, :].bitcast(I32), in_=pinv_scales.rearrange("g q c -> (g q) c").bitcast(I32))
        sort_p_scales()
        load_p(0)
        load_x(1, 0)
        load_p(1)
        load_x(0, 1)
        load_x(1, 1)
        spread_p_scales()
        for g in (1, 0):
            load_p(3 - g)
            load_x(2, g)
            load_x(3, g)
        load_d()
        nc.sync.dma_start(out=time_g[:], in_=time_gain.partition_broadcast(P))
        with nc.allow_non_contiguous_dma(reason="one gain for each partition"):
            nc.sync.dma_start(out=trace_g[:, :, 0:1], in_=trace_gain.rearrange("(i p o) -> p i o", p=P, o=1))

        for g in range(2):
            sort_p_codes(g)
            for b in range(2):
                turn_x(b, g)
                if (b, g) == (0, 0):
                    make_neg_lam()
                empty_x(b, g, nc.scalar)
            warm_up(WARM_AGAIN)
            quant_x(0, g)
        sort_p_codes(2)
        sort_p_codes(3)
        for s in range(4):
            codes_pass(s, 0)

        after = {s: [] for s in range(SLOTS)}

        def place(s, step, *args):
            after[s].append((step, args))

        for g, s in ((0, 4), (1, 2)):
            for b in (2, 3):
                place(s, turn_x, b, g)
            for b in (2, 3):
                place(s + 2, empty_x, b, g, nc.vector if (b, g) == (2, 0) else nc.scalar)
        place(10, quant_x, 1, 0)
        place(7, quant_x, 1, 1)
        for n in range(7):
            place(QUANT_H_AFTER[n], quant_h, n)
        for n in range(7):
            if QUARTERS_ON_SCALAR[n] > 0:
                place(4 * n + SCALAR_QUARTERS_AFTER[n], interleave_on_scalar, n)
            place(4 * n + 3, interleave_on_gpsimd, n)

        blocks = [(i, g) for b in range(4) for g in range(2) for i in (2 * b, 2 * b + 1)]
        for k, s in enumerate((14, 16, 18)):
            place(s, rebuild, blocks[k], 0, 2)
        for k, s in enumerate((17, 17, 18)):
            place(s, rebuild, blocks[k], 2, 3)
        for k, s in enumerate((20, 20, 21)):
            place(s, rebuild, blocks[k], 3, 4)
        for k, s in enumerate((22, 23, 24)):
            place(s, gain, blocks[k])
        for k, s in enumerate((22, 26, 26, 28, 29)):
            place(s, rebuild, blocks[3 + k], 0, 4)
        place(28, gain, blocks[3])
        place(24, round_y, blocks[0], nc.scalar)
        place(23, round_y, blocks[1], nc.gpsimd)
        place(28, round_y, blocks[2], nc.scalar)

        for s in range(-CODES_AHEAD, SLOTS):
            ahead = s + CODES_AHEAD
            if ahead < SLOTS:
                if ahead >= 4:
                    codes_pass(ahead, 0)
                codes_pass(ahead, 1)
            if 0 <= s + RELU_AHEAD < SLOTS:
                relu(s + RELU_AHEAD)
            if s >= 0:
                shrink(s)
                for step, args in after[s]:
                    step(*args)

        interleave_on_scalar(7)
        interleave_on_gpsimd(7)
        round_y(blocks[3], nc.scalar)
        gain(blocks[4])
        gain(blocks[5])
        for k in range(8, 12):
            rebuild(blocks[k], 0, 2)
        quant_h(7)
        gain(blocks[6])
        gain(blocks[7])
        round_y(blocks[4], nc.scalar)
        round_y(blocks[5], nc.scalar)
        for k in (8, 9):
            rebuild(blocks[k], 2, 3)
        for g in range(2):
            turn_y(0, 2, g)
        for k in (10, 11):
            rebuild(blocks[k], 2, 3)
        for k in range(8, 12):
            rebuild(blocks[k], 3, 4)
        for g in range(2):
            empty_y(0, 2, g)
        round_y(blocks[6], nc.gpsimd)
        round_y(blocks[7], nc.gpsimd)
        for k in range(8, 12):
            gain(blocks[k])
        round_y(blocks[8], nc.scalar)
        round_y(blocks[9], nc.gpsimd)
        rebuild(blocks[12], 0, 4)
        for g in range(2):
            turn_y(2, 2, g)
        gain(blocks[12])
        round_y(blocks[10], nc.scalar)
        round_y(blocks[11], nc.gpsimd)
        rebuild(blocks[13], 0, 4)
        rebuild(blocks[14], 0, 4)
        for g in range(2):
            empty_y(2, 2, g)
        gain(blocks[13])
        quant_y(0, 4, 0)
        store_y_codes(0, 4, 0)
        round_y(blocks[12], nc.scalar)
        gain(blocks[14])
        round_y(blocks[13], nc.scalar)
        rebuild(LAST, 0, 4)
        round_y(blocks[14], nc.gpsimd)
        quant_y(0, 4, 1)
        store_y_codes(0, 4, 1)
        store_y_scales(0, (nc.sync, nc.sync))
        pieces = [(4, 2, 0), (4, 2, 1), (6, 2, 0), (6, 1, 1), (7, 1, 1)]
        for piece in pieces[:2]:
            turn_y(*piece)
        round_last_from_psum()
        gain(LAST)
        for piece in pieces[2:]:
            turn_y(*piece)
        for piece in pieces:
            empty_y(*piece)
        for piece in pieces[:2]:
            quant_y(*piece)
        store_y_codes(4, 2, 1)
        quant_y(*pieces[2])
        store_y_codes(4, 4, 0)
        for piece in pieces[3:]:
            quant_y(*piece)
        store_y_codes(6, 2, 1)
        store_y_scales(1, (nc.scalar, nc.sync))
